import numpy as np
import ml_dtypes


def mxq(x, axis, fmt="e4m3"):
    dtype, down = {"e4m3": (ml_dtypes.float8_e4m3fn, 7), "e5m2": (ml_dtypes.float8_e5m2, 14)}[fmt]
    v = np.moveaxis(np.asarray(x, np.float32).astype(ml_dtypes.bfloat16).astype(np.float64), axis, -1)
    blocks = v.reshape(v.shape[:-1] + (-1, 32))
    amax = np.abs(blocks).max(-1, keepdims=True)
    byte = np.maximum(np.where(amax > 0, np.frexp(amax)[1] - 1 + 127, 0) - down, 1)
    scale = np.exp2(byte - 127.0)
    codes = (blocks / scale).astype(np.float32).astype(dtype).astype(np.float64)
    return np.moveaxis((codes * scale).reshape(v.shape), -1, axis)


WIDE = False


def mx_kscale(k):
    if not WIDE:
        return np.ones(k)
    levels = np.array([10, -10, 5, -5, 0])
    if k % 512:
        return np.exp2(np.random.permutation(np.resize(levels, k // 32))).repeat(32)
    a = np.empty((k // 512, 16))
    for p in range(k // 512):
        a[p, :8] = np.random.permutation(np.resize(levels, 8))
        for g in range(8):
            far = levels[np.abs(levels - a[p, g]) >= 10]
            a[p, g + 8] = far[np.random.randint(len(far))]
    return np.exp2(a.ravel()).repeat(32)


def f64(x):
    return np.asarray(x).astype(np.float64)


def striped(idx):
    return np.tile(idx.reshape(-1, 16).T, (8, 1)).astype(np.uint16)


def unstriped(offs):
    return offs[:16].T.reshape(-1).astype(np.int64)


def pack_weight(w):
    k, n = w.shape
    w = f64(np.asarray(w, np.float32).astype(ml_dtypes.bfloat16)).reshape(k // 32, 32, n)
    amax = np.abs(w).max(1)
    byte = np.clip(np.where(amax > 0, np.frexp(amax)[1] - 1 + 127 - 7, 1), 1, 254)
    scaled = (w * np.exp2(127.0 - byte)[:, None, :]).reshape(k, n).astype(np.float32)
    words = np.ascontiguousarray(scaled.reshape(k // 512, 128, 4, n).transpose(0, 1, 3, 2)).astype(ml_dtypes.float8_e4m3fn).view(np.uint8)
    return words, np.ascontiguousarray(byte.astype(np.uint8).reshape(k // 512, 16, n))


def unpack_weight(words, scales):
    g, p, n, _ = words.shape
    vals = np.ascontiguousarray(words).view(ml_dtypes.float8_e4m3fn).astype(np.float64) * np.repeat(np.exp2(scales.astype(np.float64) - 127.0), 8, axis=1)[..., None]
    return vals.transpose(0, 1, 3, 2).reshape(g * 512, n)


def relu(v):
    return np.maximum(v, 0.0)


K, T, S, H, V, W = 512, 2048, 512, 512, 512, 2048


def setup_inputs():
    n = np.random.standard_normal
    s = mx_kscale(K)[:, None]
    u = mx_kscale(H)
    packed_xT = pack_weight(n((K, T)) * s)
    packed_eT = pack_weight(n((H, W)) / np.sqrt(H) / u[:, None])
    return {
        "x_words": packed_xT[0],
        "x_scales": packed_xT[1],
        "w1": (n((K, H)) / np.sqrt(K) / s * u).astype(np.float32),
        "e_words": packed_eT[0],
        "e_scales": packed_eT[1],
        "ago": (np.random.uniform(0.0, 3.0, (S, V))).astype(np.float32),
        "before": ((np.random.uniform(size=(S, V)) < 0.6) * 1.0).astype(np.float32),
        "mu": (np.random.uniform(20.0, 80.0, (S, 1))).astype(np.float32),
        "offs": striped(np.random.permutation(T)[:S]),
        "past": striped(np.random.permutation(W)[:V]),
    }


def reference(x_words, x_scales, w1, e_words, e_scales, ago, before, mu, offs, past):
    xq = unpack_weight(x_words, x_scales)[:, unstriped(offs)]
    h = relu(mxq(f64(w1), 0, "e4m3").T @ xq)
    e_past = unpack_weight(e_words, e_scales)[:, unstriped(past)]
    y = relu(mxq(h, 0, "e4m3").T @ e_past)
    gg = (y * (np.exp(-0.7 * f64(ago)))) * f64(before)
    lam = gg.sum(axis=1, keepdims=True) + f64(mu)
    return 50.0 * (gg / lam)

@@ -1,0 +1,218 @@
+from contextlib import ExitStack
+
+import concourse.mybir as mybir
+
+F32 = mybir.dt.float32
+BF16 = mybir.dt.bfloat16
+I32 = mybir.dt.int32
+U32 = mybir.dt.uint32
+U16 = mybir.dt.uint16
+U8 = mybir.dt.uint8
+FP8X4 = mybir.dt.float8_e4m3fn_x4
+ALU = mybir.AluOpType
+ACT = mybir.ActivationFunctionType
+
+P = 128
+PACK = 4
+K, H, S, V, T = 512, 512, 512, 512, 2048
+BLOCKS = S // P
+FLOPS = 2 * K * H * S + 2 * H * S * V
+
+
+def tile_picked_yhawem_res_p_kernel(tc, x_words, x_scales, w1, e_words, e_scales, ago, before, mu, offs, past, out):
+    nc = tc.nc
+    with ExitStack() as ctx:
+        keep = ctx.enter_context(tc.tile_pool(name="keep", bufs=1))
+        share = ctx.enter_context(tc.tile_pool(name="share", bufs=1))
+        psum = ctx.enter_context(tc.psum_pool(name="psum", bufs=1))
+
+        offs_sb = keep.tile([P, S // 16], U16, name="offs_sb")
+        past_sb = keep.tile([P, V // 16], U16, name="past_sb")
+        xw = share.tile([P, T], U32, name="xw", align_bytes=64, offset=0)
+        ew = share.tile([P, T], U32, name="ew", align_bytes=64, offset=8192)
+        xs = share.tile([P, T], U8, name="xs", align_bytes=64, offset=28608)
+        es = share.tile([P, T], U8, name="es", align_bytes=64, offset=24576)
+        w_raw = keep.tile([P, PACK, H], F32, name="w_raw", align_bytes=64)
+        ago_sb = [keep.tile([P, V], F32, name=f"ago{b}", align_bytes=64) for b in range(BLOCKS)]
+        bef_sb = [keep.tile([P, V + 8], F32, name=f"bef{b}", align_bytes=64) for b in range(BLOCKS)]
+        mu_rows = keep.tile([P, 32], F32, name="mu_rows", align_bytes=64)
+        mu_cols = keep.tile([P, 32], F32, name="mu_cols", align_bytes=64)
+        warm = keep.tile([P, 8], F32, name="warm")
+
+        zero = keep.tile([P, 8], F32, name="zero")
+        nc.gpsimd.memset(zero[:], 0.0)
+        nc.gpsimd.memset(mu_rows[:], 0.0)
+        nc.vector.memset(xs[:].bitcast(I32), 0)
+        nc.vector.memset(es[:].bitcast(I32), 0)
+
+        nc.sync.dma_start(offs_sb[:], offs)
+        nc.sync.dma_start(w_raw[:], w1.rearrange("(p j) c -> p j c", j=PACK))
+        nc.scalar.dma_start(mu_rows[0:P:8, :], mu.rearrange("(b q j) o -> q b (j o)", b=BLOCKS, q=4))
+        for q in range(4):
+            nc.sync.dma_start(xs[32 * q : 32 * q + 4, :].bitcast(I32), x_scales[0, 4 * q : 4 * q + 4, :].bitcast(I32))
+        nc.sync.dma_start(xw[:].bitcast(I32), x_words[0].rearrange("p n t -> p (n t)").bitcast(I32))
+        nc.sync.dma_start(past_sb[:], past)
+        for q in range(4):
+            nc.sync.dma_start(es[32 * q : 32 * q + 4, :].bitcast(I32), e_scales[0, 4 * q : 4 * q + 4, :].bitcast(I32))
+        nc.sync.dma_start(ew[:].bitcast(I32), e_words[0].rearrange("p n t -> p (n t)").bitcast(I32))
+        for b in range(BLOCKS):
+            nc.sync.dma_start(ago_sb[b][:], ago[b * P : (b + 1) * P, :])
+            nc.sync.dma_start(bef_sb[b][:, 0:V], before[b * P : (b + 1) * P, :])
+
+        nc.scalar.activation(warm[:, 0:1], zero[:, 0:1], ACT.Exp)
+
+        xs_g = keep.tile([P, S], U8, name="xs_g", align_bytes=64)
+        es_g = share.tile([P, V], U8, name="es_g", align_bytes=64, offset=0)
+        ew_g = keep.tile([P, V], U32, name="ew_g", align_bytes=64)
+        xw_g = [share.tile([P, S // 2], U32, name=f"xw_g{u}", align_bytes=64, offset=28672 + 1024 * u) for u in range(2)]
+        w_bf = keep.tile([P, PACK, P, PACK], BF16, name="w_bf", align_bytes=64)
+        w_codes = share.tile([P, H], U32, name="w_codes", align_bytes=64, offset=26624)
+        w_scale = keep.tile([P, H], U8, name="w_scale", align_bytes=64)
+        h_ps = [psum.tile([P, PACK, P], F32, name=f"h_ps{b}") for b in range(BLOCKS)]
+        y_ps = [psum.tile([P, V], F32, name=f"y_ps{b}") for b in range(BLOCKS)]
+        h_bf = [share.tile([P, P, PACK], BF16, name=f"h_bf{b}", align_bytes=64, offset=16384 + 2048 * b) for b in range(BLOCKS)]
+        h_codes = [share.tile([P, P], U32, name=f"h_codes{b}", align_bytes=64, offset=(24576, 8192, 8704, 9216)[b]) for b in range(BLOCKS)]
+        h_scale = [keep.tile([P, P], U8, name=f"h_scale{b}", align_bytes=64) for b in range(BLOCKS)]
+        decay = [share.tile([P, V], F32, name=f"decay{b}", align_bytes=64, offset=(16384, 20480, 16384, 20480)[b]) for b in range(BLOCKS)]
+        part = [keep.tile([P, V + 8], F32, name=f"part{b}", align_bytes=64) for b in range(BLOCKS)]
+        gg = [keep.tile([P, V + 8], F32, name=f"gg{b}", align_bytes=64) for b in range(BLOCKS)]
+        res = [keep.tile([P, V], F32, name=f"res{b}", align_bytes=64) for b in range(BLOCKS)]
+        total = [keep.tile([P, 1], F32, name=f"total{b}") for b in range(BLOCKS)]
+        lam = [keep.tile([P, 1], F32, name=f"lam{b}") for b in range(BLOCKS)]
+        inv = [keep.tile([P, 1], F32, name=f"inv{b}") for b in range(BLOCKS)]
+
+        def cast():
+            src = w_raw[:].rearrange("p j (m t) -> p m j t", t=PACK)
+            dst = w_bf[:].rearrange("p t m j -> p m j t")
+            nc.vector.tensor_copy(dst[:, 0:64], src[:, 0:64])
+            nc.scalar.copy(dst[:, 64:128], src[:, 64:128])
+
+        def qw():
+            nc.vector.quantize_mx(out=w_codes[:].bitcast(FP8X4), scales=w_scale[:], in_=w_bf[:].rearrange("p t m j -> p (t m j)"))
+
+        def xsg():
+            nc.vector.tensor_copy(xs_g[:], xs[:].indirect(offs_sb[:]))
+
+        def esg():
+            nc.vector.tensor_copy(es_g[:], es[:].indirect(past_sb[:]))
+
+        def ewg():
+            nc.vector.tensor_copy(ew_g[:], ew[:].indirect(past_sb[:]))
+
+        def xg(u):
+            nc.vector.tensor_copy(xw_g[u][:], xw[:].indirect(offs_sb[:, 16 * u : 16 * (u + 1)]))
+
+        def tmu():
+            nc.vector.transpose(mu_cols[:], mu_rows[:])
+            for b in range(BLOCKS):
+                nc.gpsimd.memset(bef_sb[b][:, V : V + 1], 1.0)
+                nc.scalar.copy(part[b][:, V : V + 1], mu_cols[:, 8 * b : 8 * b + 1])
+
+        def mm1(b):
+            for t in range(PACK):
+                nc.tensor.matmul_mx(
+                    h_ps[b][:, t, :],
+                    lhsT=w_codes[:, t * P : (t + 1) * P].bitcast(FP8X4),
+                    lhsT_scale=w_scale[:, t * P : (t + 1) * P],
+                    rhs=xw_g[b // 2][:, (b % 2) * P : (b % 2 + 1) * P].bitcast(FP8X4),
+                    rhs_scale=xs_g[:, b * P : (b + 1) * P],
+                    start=True,
+                    stop=True,
+                )
+
+        def relu(b):
+            nc.scalar.activation(
+                h_bf[b][:].rearrange("p (c i) t -> p c t i", i=4), h_ps[b][:].rearrange("p t (c i) -> p c t i", i=4), ACT.Relu
+            )
+
+        def q(b):
+            nc.vector.quantize_mx(out=h_codes[b][:].bitcast(FP8X4), scales=h_scale[b][:], in_=h_bf[b][:].rearrange("p n t -> p (n t)"))
+
+        def mm2(b):
+            nc.tensor.matmul_mx(
+                y_ps[b][:],
+                lhsT=h_codes[b][:].bitcast(FP8X4),
+                lhsT_scale=h_scale[b][:],
+                rhs=ew_g[:].bitcast(FP8X4),
+                rhs_scale=es_g[:],
+                start=True,
+                stop=True,
+            )
+
+        def ex(b):
+            nc.scalar.activation(decay[b][:], ago_sb[b][:], ACT.Exp, scale=-0.7)
+
+        def e_v(b):
+            nc.vector.tensor_tensor(part[b][:], decay[b][:], bef_sb[b][:], ALU.mult)
+
+        def e_g(b):
+            nc.gpsimd.tensor_tensor(part[b][:], decay[b][:], bef_sb[b][:], ALU.mult)
+
+        def s(b):
+            nc.vector.scalar_tensor_tensor(gg[b][:], y_ps[b][:], 0.0, part[b][:], ALU.max, ALU.mult, accum_out=total[b][:])
+
+        def pa(b):
+            nc.vector.scalar_tensor_tensor(part[b][:, 0:V], y_ps[b][:], 0.0, decay[b][:], ALU.max, ALU.mult)
+
+        def pb(b):
+            nc.vector.scalar_tensor_tensor(gg[b][:, 0 : V + 1], part[b][:, 0 : V + 1], 1.0, bef_sb[b][:, 0 : V + 1], ALU.mult, ALU.mult, accum_out=total[b][:])
+
+        def la(b):
+            nc.vector.tensor_scalar(lam[b][:], total[b][:], mu_cols[:, 8 * b : 8 * b + 1], 0.02, ALU.add, ALU.mult)
+
+        def rc(b):
+            nc.vector.reciprocal(inv[b][:], total[b][:])
+
+        def f_s(b):
+            nc.scalar.activation(lam[b][:], inv[b][:], ACT.Copy, scale=50.0)
+            nc.scalar.activation(res[b][:], gg[b][:, 0:V], ACT.Copy, scale=lam[b][:])
+            nc.sync.dma_start(out[b * P : (b + 1) * P, :], res[b][:])
+
+        def f_v(b):
+            nc.vector.tensor_scalar(res[b][:], gg[b][:, 0:V], inv[b][:], 50.0, ALU.mult, ALU.mult)
+            nc.sync.dma_start(out[b * P : (b + 1) * P, :], res[b][:])
+
+        tmu()
+        cast()
+        xsg()
+        qw()
+        xg(0)
+        mm1(0)
+        relu(0)
+        mm1(1)
+        relu(1)
+        xg(1)
+        mm1(2)
+        mm1(3)
+        esg()
+        q(0)
+        ewg()
+        mm2(0)
+        ex(0)
+        relu(2)
+        relu(3)
+        q(1)
+        mm2(1)
+        q(2)
+        mm2(2)
+        q(3)
+        mm2(3)
+        pa(0)
+        ex(1)
+        pb(0)
+        pa(1)
+        rc(0)
+        f_s(0)
+        ex(2)
+        pb(1)
+        pa(2)
+        rc(1)
+        f_s(1)
+        ex(3)
+        pb(2)
+        pa(3)
+        rc(2)
+        f_s(2)
+        pb(3)
+        rc(3)
+        f_v(3)

@@ -40,20 +40,20 @@ def tile_picked_yhawem_res_p_kernel(tc, x_words, x_scales, w1, e_words, e_scales
         warm = keep.tile([P, 8], F32, name="warm")
 
         zero = keep.tile([P, 8], F32, name="zero")
-        nc.gpsimd.memset(zero[:], 0.0)
         nc.gpsimd.memset(mu_rows[:], 0.0)
         nc.vector.memset(xs[:].bitcast(I32), 0)
+        nc.gpsimd.memset(zero[:], 0.0)
         nc.vector.memset(es[:].bitcast(I32), 0)
 
         nc.sync.dma_start(offs_sb[:], offs)
         nc.sync.dma_start(w_raw[:], w1.rearrange("(p j) c -> p j c", j=PACK))
         nc.scalar.dma_start(mu_rows[0:P:8, :], mu.rearrange("(b q j) o -> q b (j o)", b=BLOCKS, q=4))
-        for q in range(4):
-            nc.sync.dma_start(xs[32 * q : 32 * q + 4, :].bitcast(I32), x_scales[0, 4 * q : 4 * q + 4, :].bitcast(I32))
+        for r in range(4):
+            nc.sync.dma_start(xs[r:P:32, :].bitcast(I32), x_scales[0, r:16:4, :].bitcast(I32))
         nc.sync.dma_start(xw[:].bitcast(I32), x_words[0].rearrange("p n t -> p (n t)").bitcast(I32))
         nc.sync.dma_start(past_sb[:], past)
-        for q in range(4):
-            nc.sync.dma_start(es[32 * q : 32 * q + 4, :].bitcast(I32), e_scales[0, 4 * q : 4 * q + 4, :].bitcast(I32))
+        for r in range(4):
+            nc.sync.dma_start(es[4 + r : P : 32, :].bitcast(I32), e_scales[0, r:16:4, :].bitcast(I32))
         nc.sync.dma_start(ew[:].bitcast(I32), e_words[0].rearrange("p n t -> p (n t)").bitcast(I32))
         for b in range(BLOCKS):
             nc.sync.dma_start(ago_sb[b][:], ago[b * P : (b + 1) * P, :])
@@ -62,8 +62,8 @@ def tile_picked_yhawem_res_p_kernel(tc, x_words, x_scales, w1, e_words, e_scales
         nc.scalar.activation(warm[:, 0:1], zero[:, 0:1], ACT.Exp)
 
         xs_g = keep.tile([P, S], U8, name="xs_g", align_bytes=64)
-        es_g = share.tile([P, V], U8, name="es_g", align_bytes=64, offset=0)
-        ew_g = keep.tile([P, V], U32, name="ew_g", align_bytes=64)
+        es_g = keep.tile([P, V], U8, name="es_g", align_bytes=64)
+        ew_g = [keep.tile([P, V // 2], U32, name=f"ew_g{u}", align_bytes=64) for u in range(2)]
         xw_g = [share.tile([P, S // 2], U32, name=f"xw_g{u}", align_bytes=64, offset=28672 + 1024 * u) for u in range(2)]
         w_bf = keep.tile([P, PACK, P, PACK], BF16, name="w_bf", align_bytes=64)
         w_codes = share.tile([P, H], U32, name="w_codes", align_bytes=64, offset=26624)
@@ -71,9 +71,9 @@ def tile_picked_yhawem_res_p_kernel(tc, x_words, x_scales, w1, e_words, e_scales
         h_ps = [psum.tile([P, PACK, P], F32, name=f"h_ps{b}") for b in range(BLOCKS)]
         y_ps = [psum.tile([P, V], F32, name=f"y_ps{b}") for b in range(BLOCKS)]
         h_bf = [share.tile([P, P, PACK], BF16, name=f"h_bf{b}", align_bytes=64, offset=16384 + 2048 * b) for b in range(BLOCKS)]
-        h_codes = [share.tile([P, P], U32, name=f"h_codes{b}", align_bytes=64, offset=(24576, 8192, 8704, 9216)[b]) for b in range(BLOCKS)]
+        decay = [share.tile([P, V], F32, name=f"decay{b}", align_bytes=64, offset=16384 + 2048 * b) for b in range(BLOCKS)]
         h_scale = [keep.tile([P, P], U8, name=f"h_scale{b}", align_bytes=64) for b in range(BLOCKS)]
-        decay = [share.tile([P, V], F32, name=f"decay{b}", align_bytes=64, offset=(16384, 20480, 16384, 20480)[b]) for b in range(BLOCKS)]
+        h_codes = [share.tile([P, P], U32, name=f"h_codes{b}", align_bytes=64, offset=(24576, 8192, 8704, 16384 + 1024)[b]) for b in range(BLOCKS)]
         part = [keep.tile([P, V + 8], F32, name=f"part{b}", align_bytes=64) for b in range(BLOCKS)]
         gg = [keep.tile([P, V + 8], F32, name=f"gg{b}", align_bytes=64) for b in range(BLOCKS)]
         res = [keep.tile([P, V], F32, name=f"res{b}", align_bytes=64) for b in range(BLOCKS)]
@@ -84,8 +84,8 @@ def tile_picked_yhawem_res_p_kernel(tc, x_words, x_scales, w1, e_words, e_scales
         def cast():
             src = w_raw[:].rearrange("p j (m t) -> p m j t", t=PACK)
             dst = w_bf[:].rearrange("p t m j -> p m j t")
-            nc.vector.tensor_copy(dst[:, 0:64], src[:, 0:64])
-            nc.scalar.copy(dst[:, 64:128], src[:, 64:128])
+            nc.vector.tensor_copy(dst[:, 0:40], src[:, 0:40])
+            nc.scalar.copy(dst[:, 40:128], src[:, 40:128])
 
         def qw():
             nc.vector.quantize_mx(out=w_codes[:].bitcast(FP8X4), scales=w_scale[:], in_=w_bf[:].rearrange("p t m j -> p (t m j)"))
@@ -96,8 +96,8 @@ def tile_picked_yhawem_res_p_kernel(tc, x_words, x_scales, w1, e_words, e_scales
         def esg():
             nc.vector.tensor_copy(es_g[:], es[:].indirect(past_sb[:]))
 
-        def ewg():
-            nc.vector.tensor_copy(ew_g[:], ew[:].indirect(past_sb[:]))
+        def ewg(u):
+            nc.vector.tensor_copy(ew_g[u][:], ew[:].indirect(past_sb[:, 16 * u : 16 * (u + 1)]))
 
         def xg(u):
             nc.vector.tensor_copy(xw_g[u][:], xw[:].indirect(offs_sb[:, 16 * u : 16 * (u + 1)]))
@@ -128,16 +128,27 @@ def tile_picked_yhawem_res_p_kernel(tc, x_words, x_scales, w1, e_words, e_scales
         def q(b):
             nc.vector.quantize_mx(out=h_codes[b][:].bitcast(FP8X4), scales=h_scale[b][:], in_=h_bf[b][:].rearrange("p n t -> p (n t)"))
 
-        def mm2(b):
+        def mm2h(b, u):
+            cols = slice(256 * u, 256 * (u + 1))
             nc.tensor.matmul_mx(
-                y_ps[b][:],
+                y_ps[b][:, cols],
                 lhsT=h_codes[b][:].bitcast(FP8X4),
                 lhsT_scale=h_scale[b][:],
-                rhs=ew_g[:].bitcast(FP8X4),
-                rhs_scale=es_g[:],
+                rhs=ew_g[u][:].bitcast(FP8X4),
+                rhs_scale=es_g[4:P, cols],
                 start=True,
                 stop=True,
             )
+
+        def mma(b):
+            mm2h(b, 0)
+
+        def mmb(b):
+            mm2h(b, 1)
+
+        def mm2(b):
+            mm2h(b, 0)
+            mm2h(b, 1)
 
         def ex(b):
             nc.scalar.activation(decay[b][:], ago_sb[b][:], ACT.Exp, scale=-0.7)
@@ -184,31 +195,33 @@ def tile_picked_yhawem_res_p_kernel(tc, x_words, x_scales, w1, e_words, e_scales
         xg(1)
         mm1(2)
         mm1(3)
-        esg()
-        q(0)
-        ewg()
-        mm2(0)
-        ex(0)
         relu(2)
         relu(3)
+        esg()
+        q(0)
+        ewg(0)
+        mma(0)
+        ewg(1)
+        mmb(0)
+        ex(0)
         q(1)
         mm2(1)
+        ex(1)
+        pa(0)
         q(2)
         mm2(2)
+        ex(2)
         q(3)
         mm2(3)
-        pa(0)
-        ex(1)
+        ex(3)
         pb(0)
         pa(1)
         rc(0)
         f_s(0)
-        ex(2)
         pb(1)
         pa(2)
         rc(1)
         f_s(1)
-        ex(3)
         pb(2)
         pa(3)
         rc(2)

@@ -33,8 +33,8 @@ def tile_picked_yhawem_res_p_kernel(tc, x_words, x_scales, w1, e_words, e_scales
         xs = share.tile([P, T], U8, name="xs", align_bytes=64, offset=28608)
         es = share.tile([P, T], U8, name="es", align_bytes=64, offset=24576)
         w_raw = keep.tile([P, PACK, H], F32, name="w_raw", align_bytes=64)
-        ago_sb = [keep.tile([P, V], F32, name=f"ago{b}", align_bytes=64) for b in range(BLOCKS)]
-        bef_sb = [keep.tile([P, V + 8], F32, name=f"bef{b}", align_bytes=64) for b in range(BLOCKS)]
+        ago_sb = [share.tile([P, V], F32, name=f"ago{b}", align_bytes=64, offset=34816 + 6144 * b) for b in range(BLOCKS)]
+        bef_sb = [keep.tile([P, V], F32, name=f"bef{b}", align_bytes=64) for b in range(BLOCKS)]
         mu_rows = keep.tile([P, 32], F32, name="mu_rows", align_bytes=64)
         mu_cols = keep.tile([P, 32], F32, name="mu_cols", align_bytes=64)
         warm = keep.tile([P, 8], F32, name="warm")
@@ -47,17 +47,22 @@ def tile_picked_yhawem_res_p_kernel(tc, x_words, x_scales, w1, e_words, e_scales
 
         nc.sync.dma_start(offs_sb[:], offs)
         nc.sync.dma_start(w_raw[:], w1.rearrange("(p j) c -> p j c", j=PACK))
-        nc.scalar.dma_start(mu_rows[0:P:8, :], mu.rearrange("(b q j) o -> q b (j o)", b=BLOCKS, q=4))
+        nc.sync.dma_start(past_sb[:], past)
         for r in range(4):
             nc.sync.dma_start(xs[r:P:32, :].bitcast(I32), x_scales[0, r:16:4, :].bitcast(I32))
         nc.sync.dma_start(xw[:].bitcast(I32), x_words[0].rearrange("p n t -> p (n t)").bitcast(I32))
-        nc.sync.dma_start(past_sb[:], past)
         for r in range(4):
             nc.sync.dma_start(es[4 + r : P : 32, :].bitcast(I32), e_scales[0, r:16:4, :].bitcast(I32))
+        nc.sync.dma_start(ago_sb[0][:], ago[0 * P : (0 + 1) * P, :])
+        nc.sync.dma_start(bef_sb[0][:], before[0 * P : (0 + 1) * P, :])
         nc.sync.dma_start(ew[:].bitcast(I32), e_words[0].rearrange("p n t -> p (n t)").bitcast(I32))
-        for b in range(BLOCKS):
-            nc.sync.dma_start(ago_sb[b][:], ago[b * P : (b + 1) * P, :])
-            nc.sync.dma_start(bef_sb[b][:, 0:V], before[b * P : (b + 1) * P, :])
+        nc.sync.dma_start(ago_sb[1][:], ago[1 * P : (1 + 1) * P, :])
+        nc.sync.dma_start(bef_sb[1][:], before[1 * P : (1 + 1) * P, :])
+        nc.sync.dma_start(mu_rows[0:P:8, :], mu.rearrange("(b q j) o -> q b (j o)", b=BLOCKS, q=4))
+        nc.sync.dma_start(bef_sb[2][:], before[2 * P : (2 + 1) * P, :])
+        nc.sync.dma_start(ago_sb[2][:], ago[2 * P : (2 + 1) * P, :])
+        nc.sync.dma_start(bef_sb[3][:], before[3 * P : (3 + 1) * P, :])
+        nc.sync.dma_start(ago_sb[3][:], ago[3 * P : (3 + 1) * P, :])
 
         nc.scalar.activation(warm[:, 0:1], zero[:, 0:1], ACT.Exp)
 
@@ -70,14 +75,19 @@ def tile_picked_yhawem_res_p_kernel(tc, x_words, x_scales, w1, e_words, e_scales
         w_scale = keep.tile([P, H], U8, name="w_scale", align_bytes=64)
         h_ps = [psum.tile([P, PACK, P], F32, name=f"h_ps{b}") for b in range(BLOCKS)]
         y_ps = [psum.tile([P, V], F32, name=f"y_ps{b}") for b in range(BLOCKS)]
-        h_bf = [share.tile([P, P, PACK], BF16, name=f"h_bf{b}", align_bytes=64, offset=16384 + 2048 * b) for b in range(BLOCKS)]
-        decay = [share.tile([P, V], F32, name=f"decay{b}", align_bytes=64, offset=16384 + 2048 * b) for b in range(BLOCKS)]
-        h_scale = [keep.tile([P, P], U8, name=f"h_scale{b}", align_bytes=64) for b in range(BLOCKS)]
-        h_codes = [share.tile([P, P], U32, name=f"h_codes{b}", align_bytes=64, offset=(24576, 8192, 8704, 16384 + 1024)[b]) for b in range(BLOCKS)]
-        part = [keep.tile([P, V + 8], F32, name=f"part{b}", align_bytes=64) for b in range(BLOCKS)]
-        gg = [keep.tile([P, V + 8], F32, name=f"gg{b}", align_bytes=64) for b in range(BLOCKS)]
-        res = [keep.tile([P, V], F32, name=f"res{b}", align_bytes=64) for b in range(BLOCKS)]
-        total = [keep.tile([P, 1], F32, name=f"total{b}") for b in range(BLOCKS)]
+        groups = [[0,1],[2,3]]
+        group_of = {b: (u, i) for u, g in enumerate(groups) for i, b in enumerate(g)}
+        h_bf = [share.tile([P, len(g) * P, PACK], BF16, name=f"h_bf{u}", align_bytes=64, offset=[36800,32832][u]) for u, g in enumerate(groups)]
+        decay = [keep.tile([P, V], F32, name=f"decay{b}", align_bytes=64) for b in range(BLOCKS)]
+        h_scale = [keep.tile([P, len(g) * P], U8, name=f"h_scale{u}", align_bytes=64) for u, g in enumerate(groups)]
+        h_codes = [share.tile([P, len(g) * P], U32, name=f"h_codes{u}", align_bytes=64, offset=[24576,8192][u]) for u, g in enumerate(groups)]
+        weight = [keep.tile([P, V], F32, name=f"weight{b}", align_bytes=64) for b in range(BLOCKS)]
+        gg = [share.tile([P, V], F32, name=f"gg{b}", align_bytes=64, offset=[61440,45120,51264,63488][b]) for b in range(BLOCKS)]
+        res = [share.tile([P, V], F32, name=f"res{b}", align_bytes=64, offset=[55232,65536,67584,69632][b]) for b in range(BLOCKS)]
+        total23 = keep.tile([P, 2], F32, name="total23")
+        lam23 = keep.tile([P, 2], F32, name="lam23")
+        inv23 = keep.tile([P, 2], F32, name="inv23")
+        total = [keep.tile([P, 1], F32, name=f"total{b}") for b in range(2)] + [total23[:, 0:1], total23[:, 1:2]]
         lam = [keep.tile([P, 1], F32, name=f"lam{b}") for b in range(BLOCKS)]
         inv = [keep.tile([P, 1], F32, name=f"inv{b}") for b in range(BLOCKS)]
 
@@ -104,9 +114,6 @@ def tile_picked_yhawem_res_p_kernel(tc, x_words, x_scales, w1, e_words, e_scales
 
         def tmu():
             nc.vector.transpose(mu_cols[:], mu_rows[:])
-            for b in range(BLOCKS):
-                nc.gpsimd.memset(bef_sb[b][:, V : V + 1], 1.0)
-                nc.scalar.copy(part[b][:, V : V + 1], mu_cols[:, 8 * b : 8 * b + 1])
 
         def mm1(b):
             for t in range(PACK):
@@ -121,111 +128,110 @@ def tile_picked_yhawem_res_p_kernel(tc, x_words, x_scales, w1, e_words, e_scales
                 )
 
         def relu(b):
+            u, i = group_of[b]
+            dst = h_bf[u][:, i * P : (i + 1) * P, :]
             nc.scalar.activation(
-                h_bf[b][:].rearrange("p (c i) t -> p c t i", i=4), h_ps[b][:].rearrange("p t (c i) -> p c t i", i=4), ACT.Relu
+                dst.rearrange("p (c i) t -> p c t i", i=4), h_ps[b][:].rearrange("p t (c i) -> p c t i", i=4), ACT.Relu
             )
 
-        def q(b):
-            nc.vector.quantize_mx(out=h_codes[b][:].bitcast(FP8X4), scales=h_scale[b][:], in_=h_bf[b][:].rearrange("p n t -> p (n t)"))
+        def q(u):
+            nc.vector.quantize_mx(out=h_codes[u][:].bitcast(FP8X4), scales=h_scale[u][:], in_=h_bf[u][:].rearrange("p n t -> p (n t)"))
 
         def mm2h(b, u):
             cols = slice(256 * u, 256 * (u + 1))
+            g, i = group_of[b]
+            rows = slice(i * P, (i + 1) * P)
             nc.tensor.matmul_mx(
                 y_ps[b][:, cols],
-                lhsT=h_codes[b][:].bitcast(FP8X4),
-                lhsT_scale=h_scale[b][:],
+                lhsT=h_codes[g][:, rows].bitcast(FP8X4),
+                lhsT_scale=h_scale[g][:, rows],
                 rhs=ew_g[u][:].bitcast(FP8X4),
                 rhs_scale=es_g[4:P, cols],
                 start=True,
                 stop=True,
             )
 
-        def mma(b):
-            mm2h(b, 0)
-
-        def mmb(b):
-            mm2h(b, 1)
-
-        def mm2(b):
-            mm2h(b, 0)
-            mm2h(b, 1)
-
         def ex(b):
             nc.scalar.activation(decay[b][:], ago_sb[b][:], ACT.Exp, scale=-0.7)
 
-        def e_v(b):
-            nc.vector.tensor_tensor(part[b][:], decay[b][:], bef_sb[b][:], ALU.mult)
-
-        def e_g(b):
-            nc.gpsimd.tensor_tensor(part[b][:], decay[b][:], bef_sb[b][:], ALU.mult)
+        def d(b):
+            nc.vector.tensor_tensor(weight[b][:], decay[b][:], bef_sb[b][:], ALU.mult)
 
         def s(b):
-            nc.vector.scalar_tensor_tensor(gg[b][:], y_ps[b][:], 0.0, part[b][:], ALU.max, ALU.mult, accum_out=total[b][:])
-
-        def pa(b):
-            nc.vector.scalar_tensor_tensor(part[b][:, 0:V], y_ps[b][:], 0.0, decay[b][:], ALU.max, ALU.mult)
-
-        def pb(b):
-            nc.vector.scalar_tensor_tensor(gg[b][:, 0 : V + 1], part[b][:, 0 : V + 1], 1.0, bef_sb[b][:, 0 : V + 1], ALU.mult, ALU.mult, accum_out=total[b][:])
+            nc.vector.scalar_tensor_tensor(gg[b][:], y_ps[b][:], 0.0, weight[b][:], ALU.max, ALU.mult, accum_out=total[b][:])
 
         def la(b):
             nc.vector.tensor_scalar(lam[b][:], total[b][:], mu_cols[:, 8 * b : 8 * b + 1], 0.02, ALU.add, ALU.mult)
 
         def rc(b):
-            nc.vector.reciprocal(inv[b][:], total[b][:])
+            nc.vector.reciprocal(inv[b][:], lam[b][:])
 
         def f_s(b):
-            nc.scalar.activation(lam[b][:], inv[b][:], ACT.Copy, scale=50.0)
-            nc.scalar.activation(res[b][:], gg[b][:, 0:V], ACT.Copy, scale=lam[b][:])
+            nc.scalar.activation(res[b][:], gg[b][:], ACT.Copy, scale=inv[b][:])
             nc.sync.dma_start(out[b * P : (b + 1) * P, :], res[b][:])
 
         def f_v(b):
-            nc.vector.tensor_scalar(res[b][:], gg[b][:, 0:V], inv[b][:], 50.0, ALU.mult, ALU.mult)
+            nc.vector.tensor_scalar(res[b][:], gg[b][:], inv[b][:], None, ALU.mult)
             nc.sync.dma_start(out[b * P : (b + 1) * P, :], res[b][:])
 
-        tmu()
+        minus_one = keep.tile([P, 8], F32, name="minus_one")
+        nc.gpsimd.memset(minus_one[:], -1.0)
+
+        def la_g(b):
+            nc.gpsimd.tensor_scalar(lam[b][:], total[b][:], mu_cols[:, 8 * b : 8 * b + 1], 0.02, ALU.add, ALU.mult)
+            nc.gpsimd.tensor_tensor(inv[b][:], lam[b][:], minus_one[:, 0:1], ALU.pow)
+
+        def la23():
+            nc.vector.tensor_tensor(lam23[:], total23[:], mu_cols[:, 16:32:8], ALU.add)
+            nc.vector.reciprocal(inv23[:], lam23[:])
+
+        def f23(b):
+            nc.vector.tensor_scalar(res[b][:], gg[b][:], inv23[:, b - 2 : b - 1], 50.0, ALU.mult, ALU.mult)
+            nc.sync.dma_start(out[b * P : (b + 1) * P, :], res[b][:])
+
         cast()
         xsg()
         qw()
         xg(0)
         mm1(0)
+        xg(1)
+        ex(0)
         relu(0)
         mm1(1)
         relu(1)
-        xg(1)
         mm1(2)
         mm1(3)
         relu(2)
         relu(3)
         esg()
+        d(0)
         q(0)
         ewg(0)
-        mma(0)
+        mm2h(0,0)
+        mm2h(1,0)
         ewg(1)
-        mmb(0)
-        ex(0)
-        q(1)
-        mm2(1)
+        mm2h(0,1)
+        mm2h(1,1)
         ex(1)
-        pa(0)
-        q(2)
-        mm2(2)
+        d(1)
+        q(1)
+        mm2h(2,0)
+        mm2h(2,1)
+        mm2h(3,0)
+        mm2h(3,1)
+        tmu()
+        s(0)
+        la_g(0)
         ex(2)
-        q(3)
-        mm2(3)
+        d(2)
+        s(1)
+        la_g(1)
         ex(3)
-        pb(0)
-        pa(1)
-        rc(0)
         f_s(0)
-        pb(1)
-        pa(2)
-        rc(1)
+        d(3)
+        s(2)
         f_s(1)
-        pb(2)
-        pa(3)
-        rc(2)
-        f_s(2)
-        pb(3)
-        rc(3)
-        f_v(3)
+        s(3)
+        la23()
+        f23(2)
+        f23(3)

@@ -33,8 +33,11 @@ def tile_picked_yhawem_res_p_kernel(tc, x_words, x_scales, w1, e_words, e_scales
         xs = share.tile([P, T], U8, name="xs", align_bytes=64, offset=28608)
         es = share.tile([P, T], U8, name="es", align_bytes=64, offset=24576)
         w_raw = keep.tile([P, PACK, H], F32, name="w_raw", align_bytes=64)
-        ago_sb = [share.tile([P, V], F32, name=f"ago{b}", align_bytes=64, offset=34816 + 6144 * b) for b in range(BLOCKS)]
-        bef_sb = [keep.tile([P, V], F32, name=f"bef{b}", align_bytes=64) for b in range(BLOCKS)]
+        ago_sb = [share.tile([P, V], F32, name=f"ago{b}", align_bytes=64, offset=34816 + 6144 * b) for b in range(2)]
+        ago_late = share.tile([P, 2, V], F32, name="ago_late", align_bytes=64, offset=34816 + 6144 * 2)
+        ago_sb = ago_sb + [ago_late[:, 0, :], ago_late[:, 1, :]]
+        bef_sb = [keep.tile([P, V], F32, name=f"bef{b}", align_bytes=64) for b in range(2)]
+        bef_late = keep.tile([P, 2, V + 8], F32, name="bef_late", align_bytes=64)
         mu_rows = keep.tile([P, 32], F32, name="mu_rows", align_bytes=64)
         mu_cols = keep.tile([P, 32], F32, name="mu_cols", align_bytes=64)
         warm = keep.tile([P, 8], F32, name="warm")
@@ -47,6 +50,7 @@ def tile_picked_yhawem_res_p_kernel(tc, x_words, x_scales, w1, e_words, e_scales
 
         nc.sync.dma_start(offs_sb[:], offs)
         nc.sync.dma_start(w_raw[:], w1.rearrange("(p j) c -> p j c", j=PACK))
+        nc.scalar.dma_start(mu_rows[0:P:8, :], mu.rearrange("(b q j) o -> q b (j o)", b=BLOCKS, q=4))
         nc.sync.dma_start(past_sb[:], past)
         for r in range(4):
             nc.sync.dma_start(xs[r:P:32, :].bitcast(I32), x_scales[0, r:16:4, :].bitcast(I32))
@@ -58,11 +62,8 @@ def tile_picked_yhawem_res_p_kernel(tc, x_words, x_scales, w1, e_words, e_scales
         nc.sync.dma_start(ew[:].bitcast(I32), e_words[0].rearrange("p n t -> p (n t)").bitcast(I32))
         nc.sync.dma_start(ago_sb[1][:], ago[1 * P : (1 + 1) * P, :])
         nc.sync.dma_start(bef_sb[1][:], before[1 * P : (1 + 1) * P, :])
-        nc.sync.dma_start(mu_rows[0:P:8, :], mu.rearrange("(b q j) o -> q b (j o)", b=BLOCKS, q=4))
-        nc.sync.dma_start(bef_sb[2][:], before[2 * P : (2 + 1) * P, :])
-        nc.sync.dma_start(ago_sb[2][:], ago[2 * P : (2 + 1) * P, :])
-        nc.sync.dma_start(bef_sb[3][:], before[3 * P : (3 + 1) * P, :])
-        nc.sync.dma_start(ago_sb[3][:], ago[3 * P : (3 + 1) * P, :])
+        nc.sync.dma_start(ago_late[:], ago[2 * P : 4 * P, :].rearrange("(b p) v -> p b v", b=2))
+        nc.sync.dma_start(bef_late[:, :, 0:V], before[2 * P : 4 * P, :].rearrange("(b p) v -> p b v", b=2))
 
         nc.scalar.activation(warm[:, 0:1], zero[:, 0:1], ACT.Exp)
 
@@ -80,14 +81,13 @@ def tile_picked_yhawem_res_p_kernel(tc, x_words, x_scales, w1, e_words, e_scales
         h_bf = [share.tile([P, len(g) * P, PACK], BF16, name=f"h_bf{u}", align_bytes=64, offset=[36800,32832][u]) for u, g in enumerate(groups)]
         decay = [keep.tile([P, V], F32, name=f"decay{b}", align_bytes=64) for b in range(BLOCKS)]
         h_scale = [keep.tile([P, len(g) * P], U8, name=f"h_scale{u}", align_bytes=64) for u, g in enumerate(groups)]
-        h_codes = [share.tile([P, len(g) * P], U32, name=f"h_codes{u}", align_bytes=64, offset=[24576,8192][u]) for u, g in enumerate(groups)]
+        h_codes = [share.tile([P, len(g) * P], U32, name=f"h_codes{u}", align_bytes=64, offset=[24576,42944][u]) for u, g in enumerate(groups)]
         weight = [keep.tile([P, V], F32, name=f"weight{b}", align_bytes=64) for b in range(BLOCKS)]
-        gg = [share.tile([P, V], F32, name=f"gg{b}", align_bytes=64, offset=[61440,45120,51264,63488][b]) for b in range(BLOCKS)]
-        res = [share.tile([P, V], F32, name=f"res{b}", align_bytes=64, offset=[55232,65536,67584,69632][b]) for b in range(BLOCKS)]
-        total23 = keep.tile([P, 2], F32, name="total23")
-        lam23 = keep.tile([P, 2], F32, name="lam23")
-        inv23 = keep.tile([P, 2], F32, name="inv23")
-        total = [keep.tile([P, 1], F32, name=f"total{b}") for b in range(2)] + [total23[:, 0:1], total23[:, 1:2]]
+        gg = [share.tile([P, V], F32, name=f"gg{b}", align_bytes=64, offset=[38976,45120,61440,63488][b]) for b in range(BLOCKS)]
+        res = [share.tile([P, V], F32, name=f"res{b}", align_bytes=64, offset=[51136,65536,67584,69632][b]) for b in range(BLOCKS)]
+        total = [keep.tile([P, 1], F32, name=f"total{b}") for b in range(BLOCKS)]
+        part = {b: keep.tile([P, V + 8], F32, name=f"part{b}", align_bytes=64) for b in (2, 3)}
+        gx = {b: keep.tile([P, V + 8], F32, name=f"gx{b}", align_bytes=64) for b in (2, 3)}
         lam = [keep.tile([P, 1], F32, name=f"lam{b}") for b in range(BLOCKS)]
         inv = [keep.tile([P, 1], F32, name=f"inv{b}") for b in range(BLOCKS)]
 
@@ -181,14 +181,29 @@ def tile_picked_yhawem_res_p_kernel(tc, x_words, x_scales, w1, e_words, e_scales
             nc.gpsimd.tensor_scalar(lam[b][:], total[b][:], mu_cols[:, 8 * b : 8 * b + 1], 0.02, ALU.add, ALU.mult)
             nc.gpsimd.tensor_tensor(inv[b][:], lam[b][:], minus_one[:, 0:1], ALU.pow)
 
-        def la23():
-            nc.vector.tensor_tensor(lam23[:], total23[:], mu_cols[:, 16:32:8], ALU.add)
-            nc.vector.reciprocal(inv23[:], lam23[:])
+        def mucol():
+            nc.gpsimd.memset(bef_late[:, :, V : V + 1], 1.0)
+            for b in (2, 3):
+                nc.gpsimd.tensor_copy(part[b][:, V : V + 1], mu_cols[:, 8 * b : 8 * b + 1])
 
-        def f23(b):
-            nc.vector.tensor_scalar(res[b][:], gg[b][:], inv23[:, b - 2 : b - 1], 50.0, ALU.mult, ALU.mult)
+        def pa(b):
+            nc.vector.scalar_tensor_tensor(part[b][:, 0:V], y_ps[b][:], 0.0, decay[b][:], ALU.max, ALU.mult)
+
+        def pb(b):
+            nc.vector.scalar_tensor_tensor(gx[b][:, 0 : V + 1], part[b][:, 0 : V + 1], 1.0, bef_late[:, b - 2, 0 : V + 1], ALU.mult, ALU.mult, accum_out=total[b][:])
+
+        def rc1(b):
+            nc.vector.reciprocal(inv[b][:], total[b][:])
+
+        def fx(b):
+            nc.vector.tensor_scalar(res[b][:], gx[b][:, 0:V], inv[b][:], 50.0, ALU.mult, ALU.mult)
             nc.sync.dma_start(out[b * P : (b + 1) * P, :], res[b][:])
 
+        def la_g1(b):
+            nc.gpsimd.tensor_scalar(lam[b][:], total[b][:], mu_cols[:, 8 * b : 8 * b + 1], 0.02, ALU.add, ALU.mult)
+
+        tmu()
+        mucol()
         cast()
         xsg()
         qw()
@@ -213,25 +228,26 @@ def tile_picked_yhawem_res_p_kernel(tc, x_words, x_scales, w1, e_words, e_scales
         mm2h(0,1)
         mm2h(1,1)
         ex(1)
-        d(1)
         q(1)
         mm2h(2,0)
         mm2h(2,1)
         mm2h(3,0)
         mm2h(3,1)
-        tmu()
         s(0)
         la_g(0)
+        d(1)
         ex(2)
-        d(2)
+        pa(2)
         s(1)
-        la_g(1)
+        la_g1(1)
         ex(3)
         f_s(0)
-        d(3)
-        s(2)
+        pa(3)
+        rc(1)
         f_s(1)
-        s(3)
-        la23()
-        f23(2)
-        f23(3)
+        pb(2)
+        pb(3)
+        rc1(2)
+        rc1(3)
+        fx(2)
+        fx(3)

@@ -33,25 +33,20 @@ def tile_picked_yhawem_res_p_kernel(tc, x_words, x_scales, w1, e_words, e_scales
         xs = share.tile([P, T], U8, name="xs", align_bytes=64, offset=28608)
         es = share.tile([P, T], U8, name="es", align_bytes=64, offset=24576)
         w_raw = keep.tile([P, PACK, H], F32, name="w_raw", align_bytes=64)
-        ago_sb = [share.tile([P, V], F32, name=f"ago{b}", align_bytes=64, offset=34816 + 6144 * b) for b in range(2)]
-        ago_late = share.tile([P, 2, V], F32, name="ago_late", align_bytes=64, offset=34816 + 6144 * 2)
-        ago_sb = ago_sb + [ago_late[:, 0, :], ago_late[:, 1, :]]
+        ago_sb = [share.tile([P, V], F32, name=f"ago{b}", align_bytes=64, offset=34816 + 6144 * b) for b in range(BLOCKS)]
         bef_sb = [keep.tile([P, V], F32, name=f"bef{b}", align_bytes=64) for b in range(2)]
         bef_late = keep.tile([P, 2, V + 8], F32, name="bef_late", align_bytes=64)
         mu_rows = keep.tile([P, 32], F32, name="mu_rows", align_bytes=64)
-        mu_cols = keep.tile([P, 32], F32, name="mu_cols", align_bytes=64)
-        warm = keep.tile([P, 8], F32, name="warm")
+        mu_cols = share.tile([P, 32], F32, name="mu_cols", align_bytes=64, offset=34816 + 1024)
 
-        zero = keep.tile([P, 8], F32, name="zero")
         nc.gpsimd.memset(mu_rows[:], 0.0)
         nc.vector.memset(xs[:].bitcast(I32), 0)
-        nc.gpsimd.memset(zero[:], 0.0)
         nc.vector.memset(es[:].bitcast(I32), 0)
 
-        nc.sync.dma_start(offs_sb[:], offs)
         nc.sync.dma_start(w_raw[:], w1.rearrange("(p j) c -> p j c", j=PACK))
-        nc.scalar.dma_start(mu_rows[0:P:8, :], mu.rearrange("(b q j) o -> q b (j o)", b=BLOCKS, q=4))
+        nc.sync.dma_start(offs_sb[:], offs)
         nc.sync.dma_start(past_sb[:], past)
+        nc.gpsimd.dma_start(mu_rows[0:P:8, :], mu.rearrange("(b q j) o -> q b (j o)", b=BLOCKS, q=4))
         for r in range(4):
             nc.sync.dma_start(xs[r:P:32, :].bitcast(I32), x_scales[0, r:16:4, :].bitcast(I32))
         nc.sync.dma_start(xw[:].bitcast(I32), x_words[0].rearrange("p n t -> p (n t)").bitcast(I32))
@@ -60,12 +55,12 @@ def tile_picked_yhawem_res_p_kernel(tc, x_words, x_scales, w1, e_words, e_scales
         nc.sync.dma_start(ago_sb[0][:], ago[0 * P : (0 + 1) * P, :])
         nc.sync.dma_start(bef_sb[0][:], before[0 * P : (0 + 1) * P, :])
         nc.sync.dma_start(ew[:].bitcast(I32), e_words[0].rearrange("p n t -> p (n t)").bitcast(I32))
-        nc.sync.dma_start(ago_sb[1][:], ago[1 * P : (1 + 1) * P, :])
         nc.sync.dma_start(bef_sb[1][:], before[1 * P : (1 + 1) * P, :])
-        nc.sync.dma_start(ago_late[:], ago[2 * P : 4 * P, :].rearrange("(b p) v -> p b v", b=2))
+        nc.sync.dma_start(ago_sb[1][:], ago[1 * P : (1 + 1) * P, :])
+        nc.sync.dma_start(ago_sb[2][:], ago[2 * P : (2 + 1) * P, :])
+        nc.sync.dma_start(ago_sb[3][:], ago[3 * P : (3 + 1) * P, :])
         nc.sync.dma_start(bef_late[:, :, 0:V], before[2 * P : 4 * P, :].rearrange("(b p) v -> p b v", b=2))
 
-        nc.scalar.activation(warm[:, 0:1], zero[:, 0:1], ACT.Exp)
 
         xs_g = keep.tile([P, S], U8, name="xs_g", align_bytes=64)
         es_g = keep.tile([P, V], U8, name="es_g", align_bytes=64)
@@ -81,10 +76,10 @@ def tile_picked_yhawem_res_p_kernel(tc, x_words, x_scales, w1, e_words, e_scales
         h_bf = [share.tile([P, len(g) * P, PACK], BF16, name=f"h_bf{u}", align_bytes=64, offset=[36800,32832][u]) for u, g in enumerate(groups)]
         decay = [keep.tile([P, V], F32, name=f"decay{b}", align_bytes=64) for b in range(BLOCKS)]
         h_scale = [keep.tile([P, len(g) * P], U8, name=f"h_scale{u}", align_bytes=64) for u, g in enumerate(groups)]
-        h_codes = [share.tile([P, len(g) * P], U32, name=f"h_codes{u}", align_bytes=64, offset=[24576,42944][u]) for u, g in enumerate(groups)]
+        h_codes = [share.tile([P, len(g) * P], U32, name=f"h_codes{u}", align_bytes=64, offset=[24576,8192][u]) for u, g in enumerate(groups)]
         weight = [keep.tile([P, V], F32, name=f"weight{b}", align_bytes=64) for b in range(BLOCKS)]
-        gg = [share.tile([P, V], F32, name=f"gg{b}", align_bytes=64, offset=[38976,45120,61440,63488][b]) for b in range(BLOCKS)]
-        res = [share.tile([P, V], F32, name=f"res{b}", align_bytes=64, offset=[51136,65536,67584,69632][b]) for b in range(BLOCKS)]
+        gg = [share.tile([P, V], F32, name=f"gg{b}", align_bytes=64, offset=[38976,42944,61440,63488][b]) for b in range(BLOCKS)]
+        res = [share.tile([P, V], F32, name=f"res{b}", align_bytes=64, offset=[55232,65536,67584,69632][b]) for b in range(BLOCKS)]
         total = [keep.tile([P, 1], F32, name=f"total{b}") for b in range(BLOCKS)]
         part = {b: keep.tile([P, V + 8], F32, name=f"part{b}", align_bytes=64) for b in (2, 3)}
         gx = {b: keep.tile([P, V + 8], F32, name=f"gx{b}", align_bytes=64) for b in (2, 3)}
@@ -94,8 +89,8 @@ def tile_picked_yhawem_res_p_kernel(tc, x_words, x_scales, w1, e_words, e_scales
         def cast():
             src = w_raw[:].rearrange("p j (m t) -> p m j t", t=PACK)
             dst = w_bf[:].rearrange("p t m j -> p m j t")
-            nc.vector.tensor_copy(dst[:, 0:40], src[:, 0:40])
-            nc.scalar.copy(dst[:, 40:128], src[:, 40:128])
+            nc.vector.tensor_copy(dst[:, 0:48], src[:, 0:48])
+            nc.scalar.copy(dst[:, 48:128], src[:, 48:128])
 
         def qw():
             nc.vector.quantize_mx(out=w_codes[:].bitcast(FP8X4), scales=w_scale[:], in_=w_bf[:].rearrange("p t m j -> p (t m j)"))
@@ -174,13 +169,6 @@ def tile_picked_yhawem_res_p_kernel(tc, x_words, x_scales, w1, e_words, e_scales
             nc.vector.tensor_scalar(res[b][:], gg[b][:], inv[b][:], None, ALU.mult)
             nc.sync.dma_start(out[b * P : (b + 1) * P, :], res[b][:])
 
-        minus_one = keep.tile([P, 8], F32, name="minus_one")
-        nc.gpsimd.memset(minus_one[:], -1.0)
-
-        def la_g(b):
-            nc.gpsimd.tensor_scalar(lam[b][:], total[b][:], mu_cols[:, 8 * b : 8 * b + 1], 0.02, ALU.add, ALU.mult)
-            nc.gpsimd.tensor_tensor(inv[b][:], lam[b][:], minus_one[:, 0:1], ALU.pow)
-
         def mucol():
             nc.gpsimd.memset(bef_late[:, :, V : V + 1], 1.0)
             for b in (2, 3):
@@ -199,11 +187,6 @@ def tile_picked_yhawem_res_p_kernel(tc, x_words, x_scales, w1, e_words, e_scales
             nc.vector.tensor_scalar(res[b][:], gx[b][:, 0:V], inv[b][:], 50.0, ALU.mult, ALU.mult)
             nc.sync.dma_start(out[b * P : (b + 1) * P, :], res[b][:])
 
-        def la_g1(b):
-            nc.gpsimd.tensor_scalar(lam[b][:], total[b][:], mu_cols[:, 8 * b : 8 * b + 1], 0.02, ALU.add, ALU.mult)
-
-        tmu()
-        mucol()
         cast()
         xsg()
         qw()
@@ -219,6 +202,8 @@ def tile_picked_yhawem_res_p_kernel(tc, x_words, x_scales, w1, e_words, e_scales
         relu(2)
         relu(3)
         esg()
+        tmu()
+        mucol()
         d(0)
         q(0)
         ewg(0)
@@ -227,20 +212,21 @@ def tile_picked_yhawem_res_p_kernel(tc, x_words, x_scales, w1, e_words, e_scales
         ewg(1)
         mm2h(0,1)
         mm2h(1,1)
-        ex(1)
         q(1)
         mm2h(2,0)
         mm2h(2,1)
         mm2h(3,0)
         mm2h(3,1)
-        s(0)
-        la_g(0)
+        ex(1)
         d(1)
-        ex(2)
-        pa(2)
+        s(0)
         s(1)
-        la_g1(1)
+        ex(2)
         ex(3)
+        la(0)
+        pa(2)
+        rc(0)
+        la(1)
         f_s(0)
         pa(3)
         rc(1)

@@ -14,9 +14,35 @@ ACT = mybir.ActivationFunctionType
 
 P = 128
 PACK = 4
+QUADRANT = 32
+LIST_ROWS = 16
 K, H, S, V, T = 512, 512, 512, 512, 2048
 BLOCKS = S // P
+HALF = 256
+EARLY = (0, 1)
+LATE = (2, 3)
+PAD = 8
+E_SCALE_ROW = 4
+MU_STEP = 8
+CAST_VECTOR = 48
+DECAY, SHARE = -0.7, 50.0
 FLOPS = 2 * K * H * S + 2 * H * S * V
+
+ROW = 4 * V
+LAP = 64
+XW_AT = 0
+EW_AT = XW_AT + 4 * T
+ES_AT = EW_AT + 4 * T
+W_CODES_AT = ES_AT + T
+XS_AT = W_CODES_AT + 4 * H - LAP
+XW_PICKED_AT = XS_AT + LAP
+AGO_AT = [XW_PICKED_AT + (2 + 3 * b) * ROW for b in range(BLOCKS)]
+BELOW, ABOVE = LAP - ROW, ROW - LAP
+H_BF_AT = [AGO_AT[0] + ABOVE, AGO_AT[0] + BELOW]
+MU_COLS_AT = AGO_AT[0] + ROW // 2
+H_CODES_AT = [ES_AT, EW_AT]
+GG_AT = [AGO_AT[1] + BELOW, AGO_AT[1] + ABOVE]
+FIRST_RESULT_AT = AGO_AT[3] + ABOVE
 
 
 def tile_picked_yhawem_res_p_kernel(tc, x_words, x_scales, w1, e_words, e_scales, ago, before, mu, offs, past, out):
@@ -26,214 +52,205 @@ def tile_picked_yhawem_res_p_kernel(tc, x_words, x_scales, w1, e_words, e_scales
         share = ctx.enter_context(tc.tile_pool(name="share", bufs=1))
         psum = ctx.enter_context(tc.psum_pool(name="psum", bufs=1))
 
-        offs_sb = keep.tile([P, S // 16], U16, name="offs_sb")
-        past_sb = keep.tile([P, V // 16], U16, name="past_sb")
-        xw = share.tile([P, T], U32, name="xw", align_bytes=64, offset=0)
-        ew = share.tile([P, T], U32, name="ew", align_bytes=64, offset=8192)
-        xs = share.tile([P, T], U8, name="xs", align_bytes=64, offset=28608)
-        es = share.tile([P, T], U8, name="es", align_bytes=64, offset=24576)
+        def events(b):
+            return slice(b * P, (b + 1) * P)
+
+        offs_sb = keep.tile([P, S // LIST_ROWS], U16, name="offs_sb")
+        past_sb = keep.tile([P, V // LIST_ROWS], U16, name="past_sb")
+        xw = share.tile([P, T], U32, name="xw", align_bytes=64, offset=XW_AT)
+        ew = share.tile([P, T], U32, name="ew", align_bytes=64, offset=EW_AT)
+        xs = share.tile([P, T], U8, name="xs", align_bytes=64, offset=XS_AT)
+        es = share.tile([P, T], U8, name="es", align_bytes=64, offset=ES_AT)
         w_raw = keep.tile([P, PACK, H], F32, name="w_raw", align_bytes=64)
-        ago_sb = [share.tile([P, V], F32, name=f"ago{b}", align_bytes=64, offset=34816 + 6144 * b) for b in range(BLOCKS)]
-        bef_sb = [keep.tile([P, V], F32, name=f"bef{b}", align_bytes=64) for b in range(2)]
-        bef_late = keep.tile([P, 2, V + 8], F32, name="bef_late", align_bytes=64)
-        mu_rows = keep.tile([P, 32], F32, name="mu_rows", align_bytes=64)
-        mu_cols = share.tile([P, 32], F32, name="mu_cols", align_bytes=64, offset=34816 + 1024)
+        ago_sb = [share.tile([P, V], F32, name=f"ago{b}", align_bytes=64, offset=AGO_AT[b]) for b in range(BLOCKS)]
+        before_early = [keep.tile([P, V], F32, name=f"before{b}", align_bytes=64) for b in EARLY]
+        before_late = keep.tile([P, len(LATE), V + PAD], F32, name="before_late", align_bytes=64)
+        mu_rows = keep.tile([P, QUADRANT], F32, name="mu_rows", align_bytes=64)
+        mu_cols = share.tile([P, QUADRANT], F32, name="mu_cols", align_bytes=64, offset=MU_COLS_AT)
 
         nc.gpsimd.memset(mu_rows[:], 0.0)
         nc.vector.memset(xs[:].bitcast(I32), 0)
         nc.vector.memset(es[:].bitcast(I32), 0)
 
+        def load_words(tile, words):
+            nc.sync.dma_start(tile[:].bitcast(I32), words[0].rearrange("p n j -> p (n j)").bitcast(I32))
+
+        def load_scales(tile, scales, first):
+            for r in range(PACK):
+                nc.sync.dma_start(tile[first + r : P : QUADRANT, :].bitcast(I32), scales[0, r : 4 * PACK : PACK, :].bitcast(I32))
+
+        def load_ago(b):
+            nc.sync.dma_start(ago_sb[b][:], ago[events(b), :])
+
+        def load_before(b):
+            nc.sync.dma_start(before_early[b][:], before[events(b), :])
+
         nc.sync.dma_start(w_raw[:], w1.rearrange("(p j) c -> p j c", j=PACK))
         nc.sync.dma_start(offs_sb[:], offs)
         nc.sync.dma_start(past_sb[:], past)
-        nc.gpsimd.dma_start(mu_rows[0:P:8, :], mu.rearrange("(b q j) o -> q b (j o)", b=BLOCKS, q=4))
-        for r in range(4):
-            nc.sync.dma_start(xs[r:P:32, :].bitcast(I32), x_scales[0, r:16:4, :].bitcast(I32))
-        nc.sync.dma_start(xw[:].bitcast(I32), x_words[0].rearrange("p n t -> p (n t)").bitcast(I32))
-        for r in range(4):
-            nc.sync.dma_start(es[4 + r : P : 32, :].bitcast(I32), e_scales[0, r:16:4, :].bitcast(I32))
-        nc.sync.dma_start(ago_sb[0][:], ago[0 * P : (0 + 1) * P, :])
-        nc.sync.dma_start(bef_sb[0][:], before[0 * P : (0 + 1) * P, :])
-        nc.sync.dma_start(ew[:].bitcast(I32), e_words[0].rearrange("p n t -> p (n t)").bitcast(I32))
-        nc.sync.dma_start(bef_sb[1][:], before[1 * P : (1 + 1) * P, :])
-        nc.sync.dma_start(ago_sb[1][:], ago[1 * P : (1 + 1) * P, :])
-        nc.sync.dma_start(ago_sb[2][:], ago[2 * P : (2 + 1) * P, :])
-        nc.sync.dma_start(ago_sb[3][:], ago[3 * P : (3 + 1) * P, :])
-        nc.sync.dma_start(bef_late[:, :, 0:V], before[2 * P : 4 * P, :].rearrange("(b p) v -> p b v", b=2))
+        nc.gpsimd.dma_start(mu_rows[0:P:MU_STEP, :], mu.rearrange("(b q j) o -> q b (j o)", b=BLOCKS, q=P // QUADRANT))
+        load_scales(xs, x_scales, 0)
+        load_words(xw, x_words)
+        load_scales(es, e_scales, E_SCALE_ROW)
+        load_ago(0)
+        load_before(0)
+        load_words(ew, e_words)
+        load_before(1)
+        for b in range(1, BLOCKS):
+            load_ago(b)
+        nc.sync.dma_start(before_late[:, :, 0:V], before[LATE[0] * P : S, :].rearrange("(b p) v -> p b v", b=len(LATE)))
 
-
-        xs_g = keep.tile([P, S], U8, name="xs_g", align_bytes=64)
-        es_g = keep.tile([P, V], U8, name="es_g", align_bytes=64)
-        ew_g = [keep.tile([P, V // 2], U32, name=f"ew_g{u}", align_bytes=64) for u in range(2)]
-        xw_g = [share.tile([P, S // 2], U32, name=f"xw_g{u}", align_bytes=64, offset=28672 + 1024 * u) for u in range(2)]
+        xs_picked = keep.tile([P, S], U8, name="xs_picked", align_bytes=64)
+        es_picked = keep.tile([P, V], U8, name="es_picked", align_bytes=64)
+        ew_picked = [keep.tile([P, HALF], U32, name=f"ew_picked{u}", align_bytes=64) for u in range(2)]
+        xw_picked = [share.tile([P, HALF], U32, name=f"xw_picked{u}", align_bytes=64, offset=XW_PICKED_AT + 4 * HALF * u) for u in range(2)]
         w_bf = keep.tile([P, PACK, P, PACK], BF16, name="w_bf", align_bytes=64)
-        w_codes = share.tile([P, H], U32, name="w_codes", align_bytes=64, offset=26624)
+        w_codes = share.tile([P, H], U32, name="w_codes", align_bytes=64, offset=W_CODES_AT)
         w_scale = keep.tile([P, H], U8, name="w_scale", align_bytes=64)
         h_ps = [psum.tile([P, PACK, P], F32, name=f"h_ps{b}") for b in range(BLOCKS)]
         y_ps = [psum.tile([P, V], F32, name=f"y_ps{b}") for b in range(BLOCKS)]
-        groups = [[0,1],[2,3]]
-        group_of = {b: (u, i) for u, g in enumerate(groups) for i, b in enumerate(g)}
-        h_bf = [share.tile([P, len(g) * P, PACK], BF16, name=f"h_bf{u}", align_bytes=64, offset=[36800,32832][u]) for u, g in enumerate(groups)]
+        h_bf = [share.tile([P, HALF, PACK], BF16, name=f"h_bf{u}", align_bytes=64, offset=H_BF_AT[u]) for u in range(2)]
+        h_scale = [keep.tile([P, HALF], U8, name=f"h_scale{u}", align_bytes=64) for u in range(2)]
+        h_codes = [share.tile([P, HALF], U32, name=f"h_codes{u}", align_bytes=64, offset=H_CODES_AT[u]) for u in range(2)]
         decay = [keep.tile([P, V], F32, name=f"decay{b}", align_bytes=64) for b in range(BLOCKS)]
-        h_scale = [keep.tile([P, len(g) * P], U8, name=f"h_scale{u}", align_bytes=64) for u, g in enumerate(groups)]
-        h_codes = [share.tile([P, len(g) * P], U32, name=f"h_codes{u}", align_bytes=64, offset=[24576,8192][u]) for u, g in enumerate(groups)]
-        weight = [keep.tile([P, V], F32, name=f"weight{b}", align_bytes=64) for b in range(BLOCKS)]
-        gg = [share.tile([P, V], F32, name=f"gg{b}", align_bytes=64, offset=[38976,42944,61440,63488][b]) for b in range(BLOCKS)]
-        res = [share.tile([P, V], F32, name=f"res{b}", align_bytes=64, offset=[55232,65536,67584,69632][b]) for b in range(BLOCKS)]
+        weight = [keep.tile([P, V], F32, name=f"weight{b}", align_bytes=64) for b in EARLY]
+        excite = {b: keep.tile([P, V + PAD], F32, name=f"excite{b}", align_bytes=64) for b in LATE}
+        gg = [share.tile([P, V], F32, name=f"gg{b}", align_bytes=64, offset=GG_AT[b]) for b in EARLY]
+        gg.extend(keep.tile([P, V + PAD], F32, name=f"gg{b}", align_bytes=64) for b in LATE)
+        result = [share.tile([P, V], F32, name="result0", align_bytes=64, offset=FIRST_RESULT_AT)]
+        result.extend(keep.tile([P, V], F32, name=f"result{b}", align_bytes=64) for b in range(1, BLOCKS))
         total = [keep.tile([P, 1], F32, name=f"total{b}") for b in range(BLOCKS)]
-        part = {b: keep.tile([P, V + 8], F32, name=f"part{b}", align_bytes=64) for b in (2, 3)}
-        gx = {b: keep.tile([P, V + 8], F32, name=f"gx{b}", align_bytes=64) for b in (2, 3)}
-        lam = [keep.tile([P, 1], F32, name=f"lam{b}") for b in range(BLOCKS)]
-        inv = [keep.tile([P, 1], F32, name=f"inv{b}") for b in range(BLOCKS)]
+        rate = [keep.tile([P, 1], F32, name=f"rate{b}") for b in EARLY]
+        inverse = [keep.tile([P, 1], F32, name=f"inverse{b}") for b in range(BLOCKS)]
 
-        def cast():
-            src = w_raw[:].rearrange("p j (m t) -> p m j t", t=PACK)
-            dst = w_bf[:].rearrange("p t m j -> p m j t")
-            nc.vector.tensor_copy(dst[:, 0:48], src[:, 0:48])
-            nc.scalar.copy(dst[:, 48:128], src[:, 48:128])
+        def gather(picked, table, offsets):
+            nc.vector.tensor_copy(picked[:], table[:].indirect(offsets))
 
-        def qw():
-            nc.vector.quantize_mx(out=w_codes[:].bitcast(FP8X4), scales=w_scale[:], in_=w_bf[:].rearrange("p t m j -> p (t m j)"))
+        def list_half(offsets, u):
+            columns = HALF // LIST_ROWS
+            return offsets[:, columns * u : columns * (u + 1)]
 
-        def xsg():
-            nc.vector.tensor_copy(xs_g[:], xs[:].indirect(offs_sb[:]))
+        def in_half(b):
+            return slice((b % 2) * P, (b % 2 + 1) * P)
 
-        def esg():
-            nc.vector.tensor_copy(es_g[:], es[:].indirect(past_sb[:]))
-
-        def ewg(u):
-            nc.vector.tensor_copy(ew_g[u][:], ew[:].indirect(past_sb[:, 16 * u : 16 * (u + 1)]))
-
-        def xg(u):
-            nc.vector.tensor_copy(xw_g[u][:], xw[:].indirect(offs_sb[:, 16 * u : 16 * (u + 1)]))
-
-        def tmu():
-            nc.vector.transpose(mu_cols[:], mu_rows[:])
-
-        def mm1(b):
+        def first_product(b):
             for t in range(PACK):
                 nc.tensor.matmul_mx(
                     h_ps[b][:, t, :],
                     lhsT=w_codes[:, t * P : (t + 1) * P].bitcast(FP8X4),
                     lhsT_scale=w_scale[:, t * P : (t + 1) * P],
-                    rhs=xw_g[b // 2][:, (b % 2) * P : (b % 2 + 1) * P].bitcast(FP8X4),
-                    rhs_scale=xs_g[:, b * P : (b + 1) * P],
+                    rhs=xw_picked[b // 2][:, in_half(b)].bitcast(FP8X4),
+                    rhs_scale=xs_picked[:, events(b)],
                     start=True,
                     stop=True,
                 )
 
         def relu(b):
-            u, i = group_of[b]
-            dst = h_bf[u][:, i * P : (i + 1) * P, :]
             nc.scalar.activation(
-                dst.rearrange("p (c i) t -> p c t i", i=4), h_ps[b][:].rearrange("p t (c i) -> p c t i", i=4), ACT.Relu
+                h_bf[b // 2][:, in_half(b), :].rearrange("p (c i) t -> p c t i", i=4),
+                h_ps[b][:].rearrange("p t (c i) -> p c t i", i=4),
+                ACT.Relu,
             )
 
-        def q(u):
+        def quantise_h(u):
             nc.vector.quantize_mx(out=h_codes[u][:].bitcast(FP8X4), scales=h_scale[u][:], in_=h_bf[u][:].rearrange("p n t -> p (n t)"))
 
-        def mm2h(b, u):
-            cols = slice(256 * u, 256 * (u + 1))
-            g, i = group_of[b]
-            rows = slice(i * P, (i + 1) * P)
+        def second_product(b, u):
+            cols = slice(HALF * u, HALF * (u + 1))
             nc.tensor.matmul_mx(
                 y_ps[b][:, cols],
-                lhsT=h_codes[g][:, rows].bitcast(FP8X4),
-                lhsT_scale=h_scale[g][:, rows],
-                rhs=ew_g[u][:].bitcast(FP8X4),
-                rhs_scale=es_g[4:P, cols],
+                lhsT=h_codes[b // 2][:, in_half(b)].bitcast(FP8X4),
+                lhsT_scale=h_scale[b // 2][:, in_half(b)],
+                rhs=ew_picked[u][:].bitcast(FP8X4),
+                rhs_scale=es_picked[E_SCALE_ROW:P, cols],
                 start=True,
                 stop=True,
             )
 
-        def ex(b):
-            nc.scalar.activation(decay[b][:], ago_sb[b][:], ACT.Exp, scale=-0.7)
+        def exp(b):
+            nc.scalar.activation(decay[b][:], ago_sb[b][:], ACT.Exp, scale=DECAY)
 
-        def d(b):
-            nc.vector.tensor_tensor(weight[b][:], decay[b][:], bef_sb[b][:], ALU.mult)
+        def early_weight(b):
+            nc.vector.tensor_tensor(weight[b][:], decay[b][:], before_early[b][:], ALU.mult)
 
-        def s(b):
+        def early_sum(b):
             nc.vector.scalar_tensor_tensor(gg[b][:], y_ps[b][:], 0.0, weight[b][:], ALU.max, ALU.mult, accum_out=total[b][:])
 
-        def la(b):
-            nc.vector.tensor_scalar(lam[b][:], total[b][:], mu_cols[:, 8 * b : 8 * b + 1], 0.02, ALU.add, ALU.mult)
+        def early_rate(b):
+            nc.vector.tensor_scalar(rate[b][:], total[b][:], mu_cols[:, MU_STEP * b : MU_STEP * b + 1], 1.0 / SHARE, ALU.add, ALU.mult)
 
-        def rc(b):
-            nc.vector.reciprocal(inv[b][:], lam[b][:])
+        def early_inverse(b):
+            nc.vector.reciprocal(inverse[b][:], rate[b][:])
 
-        def f_s(b):
-            nc.scalar.activation(res[b][:], gg[b][:], ACT.Copy, scale=inv[b][:])
-            nc.sync.dma_start(out[b * P : (b + 1) * P, :], res[b][:])
+        def early_result(b):
+            nc.scalar.activation(result[b][:], gg[b][:], ACT.Copy, scale=inverse[b][:])
+            nc.sync.dma_start(out[events(b), :], result[b][:])
 
-        def f_v(b):
-            nc.vector.tensor_scalar(res[b][:], gg[b][:], inv[b][:], None, ALU.mult)
-            nc.sync.dma_start(out[b * P : (b + 1) * P, :], res[b][:])
+        def late_excite(b):
+            nc.vector.scalar_tensor_tensor(excite[b][:, 0:V], y_ps[b][:], 0.0, decay[b][:], ALU.max, ALU.mult)
 
-        def mucol():
-            nc.gpsimd.memset(bef_late[:, :, V : V + 1], 1.0)
-            for b in (2, 3):
-                nc.gpsimd.tensor_copy(part[b][:, V : V + 1], mu_cols[:, 8 * b : 8 * b + 1])
+        def late_sum(b):
+            nc.vector.scalar_tensor_tensor(
+                gg[b][:, 0 : V + 1], excite[b][:, 0 : V + 1], 1.0, before_late[:, b - LATE[0], 0 : V + 1], ALU.mult, ALU.mult, accum_out=total[b][:]
+            )
 
-        def pa(b):
-            nc.vector.scalar_tensor_tensor(part[b][:, 0:V], y_ps[b][:], 0.0, decay[b][:], ALU.max, ALU.mult)
+        def late_result(b):
+            nc.vector.tensor_scalar(result[b][:], gg[b][:, 0:V], inverse[b][:], SHARE, ALU.mult, ALU.mult)
+            nc.sync.dma_start(out[events(b), :], result[b][:])
 
-        def pb(b):
-            nc.vector.scalar_tensor_tensor(gx[b][:, 0 : V + 1], part[b][:, 0 : V + 1], 1.0, bef_late[:, b - 2, 0 : V + 1], ALU.mult, ALU.mult, accum_out=total[b][:])
+        w_src = w_raw[:].rearrange("p j (m t) -> p m j t", t=PACK)
+        w_dst = w_bf[:].rearrange("p t m j -> p m j t")
+        nc.vector.tensor_copy(w_dst[:, 0:CAST_VECTOR], w_src[:, 0:CAST_VECTOR])
+        nc.scalar.copy(w_dst[:, CAST_VECTOR:P], w_src[:, CAST_VECTOR:P])
+        gather(xs_picked, xs, offs_sb[:])
+        nc.vector.quantize_mx(out=w_codes[:].bitcast(FP8X4), scales=w_scale[:], in_=w_bf[:].rearrange("p t m j -> p (t m j)"))
 
-        def rc1(b):
-            nc.vector.reciprocal(inv[b][:], total[b][:])
-
-        def fx(b):
-            nc.vector.tensor_scalar(res[b][:], gx[b][:, 0:V], inv[b][:], 50.0, ALU.mult, ALU.mult)
-            nc.sync.dma_start(out[b * P : (b + 1) * P, :], res[b][:])
-
-        cast()
-        xsg()
-        qw()
-        xg(0)
-        mm1(0)
-        xg(1)
-        ex(0)
+        gather(xw_picked[0], xw, list_half(offs_sb, 0))
+        first_product(0)
+        gather(xw_picked[1], xw, list_half(offs_sb, 1))
+        exp(0)
         relu(0)
-        mm1(1)
+        first_product(1)
         relu(1)
-        mm1(2)
-        mm1(3)
-        relu(2)
-        relu(3)
-        esg()
-        tmu()
-        mucol()
-        d(0)
-        q(0)
-        ewg(0)
-        mm2h(0,0)
-        mm2h(1,0)
-        ewg(1)
-        mm2h(0,1)
-        mm2h(1,1)
-        q(1)
-        mm2h(2,0)
-        mm2h(2,1)
-        mm2h(3,0)
-        mm2h(3,1)
-        ex(1)
-        d(1)
-        s(0)
-        s(1)
-        ex(2)
-        ex(3)
-        la(0)
-        pa(2)
-        rc(0)
-        la(1)
-        f_s(0)
-        pa(3)
-        rc(1)
-        f_s(1)
-        pb(2)
-        pb(3)
-        rc1(2)
-        rc1(3)
-        fx(2)
-        fx(3)
+        for b in LATE:
+            first_product(b)
+        for b in LATE:
+            relu(b)
+
+        gather(es_picked, es, past_sb[:])
+        nc.vector.transpose(mu_cols[:], mu_rows[:])
+        nc.gpsimd.memset(before_late[:, :, V : V + 1], 1.0)
+        for b in LATE:
+            nc.gpsimd.tensor_copy(excite[b][:, V : V + 1], mu_cols[:, MU_STEP * b : MU_STEP * b + 1])
+        early_weight(0)
+        quantise_h(0)
+
+        for u in range(2):
+            gather(ew_picked[u], ew, list_half(past_sb, u))
+            for b in EARLY:
+                second_product(b, u)
+        quantise_h(1)
+        for b in LATE:
+            for u in range(2):
+                second_product(b, u)
+
+        exp(1)
+        early_weight(1)
+        for b in EARLY:
+            early_sum(b)
+        for b in LATE:
+            exp(b)
+        early_rate(0)
+        late_excite(2)
+        early_inverse(0)
+        early_rate(1)
+        early_result(0)
+        late_excite(3)
+        early_inverse(1)
+        early_result(1)
+        for b in LATE:
+            late_sum(b)
+        for b in LATE:
+            nc.vector.reciprocal(inverse[b][:], total[b][:])
+        for b in LATE:
+            late_result(b)

@@ -15,6 +15,8 @@ ACT = mybir.ActivationFunctionType
 P = 128
 PACK = 4
 QUADRANT = 32
+QUADRANT_SCALES = 4
+SCALE_ROWS = QUADRANT_SCALES * P // QUADRANT
 LIST_ROWS = 16
 K, H, S, V, T = 512, 512, 512, 512, 2048
 BLOCKS = S // P
@@ -25,7 +27,7 @@ PAD = 8
 E_SCALE_ROW = 4
 MU_STEP = 8
 CAST_VECTOR = 48
-DECAY, SHARE = -0.7, 50.0
+DECAY_RATE, OUT_FACTOR = -0.7, 50.0
 FLOPS = 2 * K * H * S + 2 * H * S * V
 
 ROW = 4 * V
@@ -36,13 +38,9 @@ ES_AT = EW_AT + 4 * T
 W_CODES_AT = ES_AT + T
 XS_AT = W_CODES_AT + 4 * H - LAP
 XW_PICKED_AT = XS_AT + LAP
-AGO_AT = [XW_PICKED_AT + (2 + 3 * b) * ROW for b in range(BLOCKS)]
-BELOW, ABOVE = LAP - ROW, ROW - LAP
-H_BF_AT = [AGO_AT[0] + ABOVE, AGO_AT[0] + BELOW]
-MU_COLS_AT = AGO_AT[0] + ROW // 2
-H_CODES_AT = [ES_AT, EW_AT]
-GG_AT = [AGO_AT[1] + BELOW, AGO_AT[1] + ABOVE]
-FIRST_RESULT_AT = AGO_AT[3] + ABOVE
+H_CODES_AT = EW_AT
+LAST_AGO_AT = XW_PICKED_AT + ROW
+FIRST_RESULT_AT = LAST_AGO_AT
 
 
 def tile_picked_yhawem_res_p_kernel(tc, x_words, x_scales, w1, e_words, e_scales, ago, before, mu, offs, past, out):
@@ -62,11 +60,12 @@ def tile_picked_yhawem_res_p_kernel(tc, x_words, x_scales, w1, e_words, e_scales
         xs = share.tile([P, T], U8, name="xs", align_bytes=64, offset=XS_AT)
         es = share.tile([P, T], U8, name="es", align_bytes=64, offset=ES_AT)
         w_raw = keep.tile([P, PACK, H], F32, name="w_raw", align_bytes=64)
-        ago_sb = [share.tile([P, V], F32, name=f"ago{b}", align_bytes=64, offset=AGO_AT[b]) for b in range(BLOCKS)]
-        before_early = [keep.tile([P, V], F32, name=f"before{b}", align_bytes=64) for b in EARLY]
+        ago_sb = [keep.tile([P, V], F32, name=f"ago{b}", align_bytes=64) for b in range(BLOCKS - 1)]
+        ago_sb.append(share.tile([P, V], F32, name="ago_last", align_bytes=64, offset=LAST_AGO_AT))
+        before_early = keep.tile([P, len(EARLY), V], F32, name="before_early", align_bytes=64)
         before_late = keep.tile([P, len(LATE), V + PAD], F32, name="before_late", align_bytes=64)
         mu_rows = keep.tile([P, QUADRANT], F32, name="mu_rows", align_bytes=64)
-        mu_cols = share.tile([P, QUADRANT], F32, name="mu_cols", align_bytes=64, offset=MU_COLS_AT)
+        mu_cols = keep.tile([P, QUADRANT], F32, name="mu_cols", align_bytes=64)
 
         nc.gpsimd.memset(mu_rows[:], 0.0)
         nc.vector.memset(xs[:].bitcast(I32), 0)
@@ -76,47 +75,44 @@ def tile_picked_yhawem_res_p_kernel(tc, x_words, x_scales, w1, e_words, e_scales
             nc.sync.dma_start(tile[:].bitcast(I32), words[0].rearrange("p n j -> p (n j)").bitcast(I32))
 
         def load_scales(tile, scales, first):
-            for r in range(PACK):
-                nc.sync.dma_start(tile[first + r : P : QUADRANT, :].bitcast(I32), scales[0, r : 4 * PACK : PACK, :].bitcast(I32))
+            for r in range(QUADRANT_SCALES):
+                nc.sync.dma_start(tile[first + r : P : QUADRANT, :].bitcast(I32), scales[0, r:SCALE_ROWS:QUADRANT_SCALES, :].bitcast(I32))
 
         def load_ago(b):
             nc.sync.dma_start(ago_sb[b][:], ago[events(b), :])
 
-        def load_before(b):
-            nc.sync.dma_start(before_early[b][:], before[events(b), :])
+        def load_before(tile, blocks):
+            nc.sync.dma_start(tile[:, :, 0:V], before[blocks[0] * P : (blocks[-1] + 1) * P, :].rearrange("(b p) v -> p b v", b=len(blocks)))
 
         nc.sync.dma_start(w_raw[:], w1.rearrange("(p j) c -> p j c", j=PACK))
         nc.sync.dma_start(offs_sb[:], offs)
         nc.sync.dma_start(past_sb[:], past)
-        nc.gpsimd.dma_start(mu_rows[0:P:MU_STEP, :], mu.rearrange("(b q j) o -> q b (j o)", b=BLOCKS, q=P // QUADRANT))
         load_scales(xs, x_scales, 0)
         load_words(xw, x_words)
+        nc.sync.dma_start(mu_rows[0:P:MU_STEP, :], mu.rearrange("(b q j) o -> q b (j o)", b=BLOCKS, q=P // QUADRANT))
         load_scales(es, e_scales, E_SCALE_ROW)
-        load_ago(0)
-        load_before(0)
         load_words(ew, e_words)
-        load_before(1)
-        for b in range(1, BLOCKS):
-            load_ago(b)
-        nc.sync.dma_start(before_late[:, :, 0:V], before[LATE[0] * P : S, :].rearrange("(b p) v -> p b v", b=len(LATE)))
+        for blocks, tile in ((EARLY, before_early), (LATE, before_late)):
+            for b in blocks:
+                load_ago(b)
+            load_before(tile, blocks)
 
         xs_picked = keep.tile([P, S], U8, name="xs_picked", align_bytes=64)
         es_picked = keep.tile([P, V], U8, name="es_picked", align_bytes=64)
-        ew_picked = [keep.tile([P, HALF], U32, name=f"ew_picked{u}", align_bytes=64) for u in range(2)]
+        ew_picked = keep.tile([P, V], U32, name="ew_picked", align_bytes=64)
         xw_picked = [share.tile([P, HALF], U32, name=f"xw_picked{u}", align_bytes=64, offset=XW_PICKED_AT + 4 * HALF * u) for u in range(2)]
         w_bf = keep.tile([P, PACK, P, PACK], BF16, name="w_bf", align_bytes=64)
         w_codes = share.tile([P, H], U32, name="w_codes", align_bytes=64, offset=W_CODES_AT)
         w_scale = keep.tile([P, H], U8, name="w_scale", align_bytes=64)
         h_ps = [psum.tile([P, PACK, P], F32, name=f"h_ps{b}") for b in range(BLOCKS)]
         y_ps = [psum.tile([P, V], F32, name=f"y_ps{b}") for b in range(BLOCKS)]
-        h_bf = [share.tile([P, HALF, PACK], BF16, name=f"h_bf{u}", align_bytes=64, offset=H_BF_AT[u]) for u in range(2)]
+        h_bf = [keep.tile([P, HALF, PACK], BF16, name=f"h_bf{u}", align_bytes=64) for u in range(2)]
         h_scale = [keep.tile([P, HALF], U8, name=f"h_scale{u}", align_bytes=64) for u in range(2)]
-        h_codes = [share.tile([P, HALF], U32, name=f"h_codes{u}", align_bytes=64, offset=H_CODES_AT[u]) for u in range(2)]
+        h_codes = [share.tile([P, HALF], U32, name=f"h_codes{u}", align_bytes=64, offset=H_CODES_AT + 4 * HALF * u) for u in range(2)]
         decay = [keep.tile([P, V], F32, name=f"decay{b}", align_bytes=64) for b in range(BLOCKS)]
         weight = [keep.tile([P, V], F32, name=f"weight{b}", align_bytes=64) for b in EARLY]
         excite = {b: keep.tile([P, V + PAD], F32, name=f"excite{b}", align_bytes=64) for b in LATE}
-        gg = [share.tile([P, V], F32, name=f"gg{b}", align_bytes=64, offset=GG_AT[b]) for b in EARLY]
-        gg.extend(keep.tile([P, V + PAD], F32, name=f"gg{b}", align_bytes=64) for b in LATE)
+        gg = [keep.tile([P, V + PAD], F32, name=f"gg{b}", align_bytes=64) for b in range(BLOCKS)]
         result = [share.tile([P, V], F32, name="result0", align_bytes=64, offset=FIRST_RESULT_AT)]
         result.extend(keep.tile([P, V], F32, name=f"result{b}", align_bytes=64) for b in range(1, BLOCKS))
         total = [keep.tile([P, 1], F32, name=f"total{b}") for b in range(BLOCKS)]
@@ -125,10 +121,6 @@ def tile_picked_yhawem_res_p_kernel(tc, x_words, x_scales, w1, e_words, e_scales
 
         def gather(picked, table, offsets):
             nc.vector.tensor_copy(picked[:], table[:].indirect(offsets))
-
-        def list_half(offsets, u):
-            columns = HALF // LIST_ROWS
-            return offsets[:, columns * u : columns * (u + 1)]
 
         def in_half(b):
             return slice((b % 2) * P, (b % 2 + 1) * P)
@@ -155,35 +147,34 @@ def tile_picked_yhawem_res_p_kernel(tc, x_words, x_scales, w1, e_words, e_scales
         def quantise_h(u):
             nc.vector.quantize_mx(out=h_codes[u][:].bitcast(FP8X4), scales=h_scale[u][:], in_=h_bf[u][:].rearrange("p n t -> p (n t)"))
 
-        def second_product(b, u):
-            cols = slice(HALF * u, HALF * (u + 1))
+        def second_product(b):
             nc.tensor.matmul_mx(
-                y_ps[b][:, cols],
+                y_ps[b][:],
                 lhsT=h_codes[b // 2][:, in_half(b)].bitcast(FP8X4),
                 lhsT_scale=h_scale[b // 2][:, in_half(b)],
-                rhs=ew_picked[u][:].bitcast(FP8X4),
-                rhs_scale=es_picked[E_SCALE_ROW:P, cols],
+                rhs=ew_picked[:].bitcast(FP8X4),
+                rhs_scale=es_picked[E_SCALE_ROW:P, :],
                 start=True,
                 stop=True,
             )
 
         def exp(b):
-            nc.scalar.activation(decay[b][:], ago_sb[b][:], ACT.Exp, scale=DECAY)
+            nc.scalar.activation(decay[b][:], ago_sb[b][:], ACT.Exp, scale=DECAY_RATE)
 
         def early_weight(b):
-            nc.vector.tensor_tensor(weight[b][:], decay[b][:], before_early[b][:], ALU.mult)
+            nc.vector.tensor_tensor(weight[b][:], decay[b][:], before_early[:, b, :], ALU.mult)
 
         def early_sum(b):
-            nc.vector.scalar_tensor_tensor(gg[b][:], y_ps[b][:], 0.0, weight[b][:], ALU.max, ALU.mult, accum_out=total[b][:])
+            nc.vector.scalar_tensor_tensor(gg[b][:, 0:V], y_ps[b][:], 0.0, weight[b][:], ALU.max, ALU.mult, accum_out=total[b][:])
 
         def early_rate(b):
-            nc.vector.tensor_scalar(rate[b][:], total[b][:], mu_cols[:, MU_STEP * b : MU_STEP * b + 1], 1.0 / SHARE, ALU.add, ALU.mult)
+            nc.vector.tensor_scalar(rate[b][:], total[b][:], mu_cols[:, MU_STEP * b : MU_STEP * b + 1], 1.0 / OUT_FACTOR, ALU.add, ALU.mult)
 
         def early_inverse(b):
             nc.vector.reciprocal(inverse[b][:], rate[b][:])
 
         def early_result(b):
-            nc.scalar.activation(result[b][:], gg[b][:], ACT.Copy, scale=inverse[b][:])
+            nc.scalar.activation(result[b][:], gg[b][:, 0:V], ACT.Copy, scale=inverse[b][:])
             nc.sync.dma_start(out[events(b), :], result[b][:])
 
         def late_excite(b):
@@ -195,7 +186,7 @@ def tile_picked_yhawem_res_p_kernel(tc, x_words, x_scales, w1, e_words, e_scales
             )
 
         def late_result(b):
-            nc.vector.tensor_scalar(result[b][:], gg[b][:, 0:V], inverse[b][:], SHARE, ALU.mult, ALU.mult)
+            nc.vector.tensor_scalar(result[b][:], gg[b][:, 0:V], inverse[b][:], OUT_FACTOR, ALU.mult, ALU.mult)
             nc.sync.dma_start(out[events(b), :], result[b][:])
 
         w_src = w_raw[:].rearrange("p j (m t) -> p m j t", t=PACK)
@@ -205,41 +196,30 @@ def tile_picked_yhawem_res_p_kernel(tc, x_words, x_scales, w1, e_words, e_scales
         gather(xs_picked, xs, offs_sb[:])
         nc.vector.quantize_mx(out=w_codes[:].bitcast(FP8X4), scales=w_scale[:], in_=w_bf[:].rearrange("p t m j -> p (t m j)"))
 
-        gather(xw_picked[0], xw, list_half(offs_sb, 0))
-        first_product(0)
-        gather(xw_picked[1], xw, list_half(offs_sb, 1))
-        exp(0)
-        relu(0)
-        first_product(1)
-        relu(1)
-        for b in LATE:
+        for u in range(2):
+            gather(xw_picked[u], xw, offs_sb[:, u * HALF // LIST_ROWS : (u + 1) * HALF // LIST_ROWS])
+        for b in range(BLOCKS):
             first_product(b)
-        for b in LATE:
             relu(b)
 
-        gather(es_picked, es, past_sb[:])
         nc.vector.transpose(mu_cols[:], mu_rows[:])
         nc.gpsimd.memset(before_late[:, :, V : V + 1], 1.0)
         for b in LATE:
             nc.gpsimd.tensor_copy(excite[b][:, V : V + 1], mu_cols[:, MU_STEP * b : MU_STEP * b + 1])
-        early_weight(0)
-        quantise_h(0)
 
+        gather(es_picked, es, past_sb[:])
+        gather(ew_picked, ew, past_sb[:])
         for u in range(2):
-            gather(ew_picked[u], ew, list_half(past_sb, u))
-            for b in EARLY:
-                second_product(b, u)
-        quantise_h(1)
-        for b in LATE:
-            for u in range(2):
-                second_product(b, u)
+            quantise_h(u)
+        for b in range(BLOCKS):
+            second_product(b)
 
-        exp(1)
-        early_weight(1)
+        for b in range(BLOCKS):
+            exp(b)
+        for b in EARLY:
+            early_weight(b)
         for b in EARLY:
             early_sum(b)
-        for b in LATE:
-            exp(b)
         early_rate(0)
         late_excite(2)
         early_inverse(0)

@@ -17,16 +17,14 @@ PACK = 4
 QUADRANT = 32
 QUADRANT_SCALES = 4
 SCALE_ROWS = QUADRANT_SCALES * P // QUADRANT
+WIDE_AT = P - SCALE_ROWS
 LIST_ROWS = 16
 K, H, S, V, T = 512, 512, 512, 512, 2048
 BLOCKS = S // P
 HALF = 256
-EARLY = (0, 1)
-LATE = (2, 3)
 PAD = 8
-E_SCALE_ROW = 4
 MU_STEP = 8
-CAST_VECTOR = 48
+CAST_VECTOR = 88
 DECAY_RATE, OUT_FACTOR = -0.7, 50.0
 FLOPS = 2 * K * H * S + 2 * H * S * V
 
@@ -34,13 +32,13 @@ ROW = 4 * V
 LAP = 64
 XW_AT = 0
 EW_AT = XW_AT + 4 * T
-ES_AT = EW_AT + 4 * T
-W_CODES_AT = ES_AT + T
-XS_AT = W_CODES_AT + 4 * H - LAP
-XW_PICKED_AT = XS_AT + LAP
-H_CODES_AT = EW_AT
-LAST_AGO_AT = XW_PICKED_AT + ROW
-FIRST_RESULT_AT = LAST_AGO_AT
+W_CODES_AT = EW_AT + 4 * T
+ES_AT = W_CODES_AT + 4 * H
+XW_PICKED_AT = ES_AT + T
+H_CODES_AT = XW_PICKED_AT + ROW
+ES_PICKED_AT = H_CODES_AT + 4 * S - LAP
+AGO_AT = ES_PICKED_AT + V
+EXCITE_AT = AGO_AT + BLOCKS * ROW
 
 
 def tile_picked_yhawem_res_p_kernel(tc, x_words, x_scales, w1, e_words, e_scales, ago, before, mu, offs, past, out):
@@ -57,48 +55,17 @@ def tile_picked_yhawem_res_p_kernel(tc, x_words, x_scales, w1, e_words, e_scales
         past_sb = keep.tile([P, V // LIST_ROWS], U16, name="past_sb")
         xw = share.tile([P, T], U32, name="xw", align_bytes=64, offset=XW_AT)
         ew = share.tile([P, T], U32, name="ew", align_bytes=64, offset=EW_AT)
-        xs = share.tile([P, T], U8, name="xs", align_bytes=64, offset=XS_AT)
+        xs = keep.tile([P, T], U8, name="xs", align_bytes=64)
         es = share.tile([P, T], U8, name="es", align_bytes=64, offset=ES_AT)
         w_raw = keep.tile([P, PACK, H], F32, name="w_raw", align_bytes=64)
-        ago_sb = [keep.tile([P, V], F32, name=f"ago{b}", align_bytes=64) for b in range(BLOCKS - 1)]
-        ago_sb.append(share.tile([P, V], F32, name="ago_last", align_bytes=64, offset=LAST_AGO_AT))
-        before_early = keep.tile([P, len(EARLY), V], F32, name="before_early", align_bytes=64)
-        before_late = keep.tile([P, len(LATE), V + PAD], F32, name="before_late", align_bytes=64)
+        ago_sb = [share.tile([P, V], F32, name=f"ago{b}", align_bytes=64, offset=AGO_AT + ROW * b) for b in range(BLOCKS)]
+        before_sb = keep.tile([P, BLOCKS, V + PAD], F32, name="before_sb", align_bytes=64)
         mu_rows = keep.tile([P, QUADRANT], F32, name="mu_rows", align_bytes=64)
-        mu_cols = keep.tile([P, QUADRANT], F32, name="mu_cols", align_bytes=64)
-
-        nc.gpsimd.memset(mu_rows[:], 0.0)
-        nc.vector.memset(xs[:].bitcast(I32), 0)
-        nc.vector.memset(es[:].bitcast(I32), 0)
-
-        def load_words(tile, words):
-            nc.sync.dma_start(tile[:].bitcast(I32), words[0].rearrange("p n j -> p (n j)").bitcast(I32))
-
-        def load_scales(tile, scales, first):
-            for r in range(QUADRANT_SCALES):
-                nc.sync.dma_start(tile[first + r : P : QUADRANT, :].bitcast(I32), scales[0, r:SCALE_ROWS:QUADRANT_SCALES, :].bitcast(I32))
-
-        def load_ago(b):
-            nc.sync.dma_start(ago_sb[b][:], ago[events(b), :])
-
-        def load_before(tile, blocks):
-            nc.sync.dma_start(tile[:, :, 0:V], before[blocks[0] * P : (blocks[-1] + 1) * P, :].rearrange("(b p) v -> p b v", b=len(blocks)))
-
-        nc.sync.dma_start(w_raw[:], w1.rearrange("(p j) c -> p j c", j=PACK))
-        nc.sync.dma_start(offs_sb[:], offs)
-        nc.sync.dma_start(past_sb[:], past)
-        load_scales(xs, x_scales, 0)
-        load_words(xw, x_words)
-        nc.sync.dma_start(mu_rows[0:P:MU_STEP, :], mu.rearrange("(b q j) o -> q b (j o)", b=BLOCKS, q=P // QUADRANT))
-        load_scales(es, e_scales, E_SCALE_ROW)
-        load_words(ew, e_words)
-        for blocks, tile in ((EARLY, before_early), (LATE, before_late)):
-            for b in blocks:
-                load_ago(b)
-            load_before(tile, blocks)
-
+        mu_cols = share.tile([P, QUADRANT], F32, name="mu_cols", align_bytes=64, offset=ES_AT)
         xs_picked = keep.tile([P, S], U8, name="xs_picked", align_bytes=64)
-        es_picked = keep.tile([P, V], U8, name="es_picked", align_bytes=64)
+        es_picked = share.tile([P, V], U8, name="es_picked", align_bytes=64, offset=ES_PICKED_AT)
+        xs_plane = keep.tile([P, S], U8, name="xs_plane", align_bytes=64)
+        es_plane = keep.tile([P, V], U8, name="es_plane", align_bytes=64)
         ew_picked = keep.tile([P, V], U32, name="ew_picked", align_bytes=64)
         xw_picked = [share.tile([P, HALF], U32, name=f"xw_picked{u}", align_bytes=64, offset=XW_PICKED_AT + 4 * HALF * u) for u in range(2)]
         w_bf = keep.tile([P, PACK, P, PACK], BF16, name="w_bf", align_bytes=64)
@@ -106,18 +73,52 @@ def tile_picked_yhawem_res_p_kernel(tc, x_words, x_scales, w1, e_words, e_scales
         w_scale = keep.tile([P, H], U8, name="w_scale", align_bytes=64)
         h_ps = [psum.tile([P, PACK, P], F32, name=f"h_ps{b}") for b in range(BLOCKS)]
         y_ps = [psum.tile([P, V], F32, name=f"y_ps{b}") for b in range(BLOCKS)]
-        h_bf = [keep.tile([P, HALF, PACK], BF16, name=f"h_bf{u}", align_bytes=64) for u in range(2)]
-        h_scale = [keep.tile([P, HALF], U8, name=f"h_scale{u}", align_bytes=64) for u in range(2)]
-        h_codes = [share.tile([P, HALF], U32, name=f"h_codes{u}", align_bytes=64, offset=H_CODES_AT + 4 * HALF * u) for u in range(2)]
-        decay = [keep.tile([P, V], F32, name=f"decay{b}", align_bytes=64) for b in range(BLOCKS)]
-        weight = [keep.tile([P, V], F32, name=f"weight{b}", align_bytes=64) for b in EARLY]
-        excite = {b: keep.tile([P, V + PAD], F32, name=f"excite{b}", align_bytes=64) for b in LATE}
-        gg = [keep.tile([P, V + PAD], F32, name=f"gg{b}", align_bytes=64) for b in range(BLOCKS)]
-        result = [share.tile([P, V], F32, name="result0", align_bytes=64, offset=FIRST_RESULT_AT)]
-        result.extend(keep.tile([P, V], F32, name=f"result{b}", align_bytes=64) for b in range(1, BLOCKS))
-        total = [keep.tile([P, 1], F32, name=f"total{b}") for b in range(BLOCKS)]
-        rate = [keep.tile([P, 1], F32, name=f"rate{b}") for b in EARLY]
+        h_bf = keep.tile([P, S, PACK], BF16, name="h_bf", align_bytes=64)
+        h_scale = keep.tile([P, S], U8, name="h_scale", align_bytes=64)
+        h_codes = share.tile([P, S], U32, name="h_codes", align_bytes=64, offset=H_CODES_AT)
+        decay = [
+            share.tile([P, V], F32, name="decay0", align_bytes=64, offset=W_CODES_AT),
+            share.tile([P, V], F32, name="decay1", align_bytes=64, offset=XW_PICKED_AT),
+            keep.tile([P, V], F32, name="decay2", align_bytes=64),
+            keep.tile([P, V], F32, name="decay3", align_bytes=64),
+        ]
+        weight = keep.tile([P, V], F32, name="weight", align_bytes=64)
+        mu_part = keep.tile([P, 2], F32, name="mu_part")
+        rate = [share.tile([P, 1], F32, name=f"rate{b}", align_bytes=64, offset=AGO_AT + 3 * ROW + LAP * b) for b in range(2)]
+        excite = {1: keep.tile([P, V], F32, name="excite1", align_bytes=64)}
+        excite.setdefault(2, keep.tile([P, V + PAD], F32, name="excite2", align_bytes=64))
+        excite.setdefault(3, share.tile([P, V + PAD], F32, name="excite3", align_bytes=64, offset=EXCITE_AT + ROW + LAP))
+        minus_one = keep.tile([P, 1], F32, name="minus_one")
+        nc.gpsimd.memset(minus_one[:], -1.0)
+        gg = [share.tile([P, V], F32, name="gg0", align_bytes=64, offset=AGO_AT + ROW)]
+        gg.extend(keep.tile([P, V + PAD], F32, name=f"gg{b}", align_bytes=64) for b in range(1, BLOCKS))
+        result = [keep.tile([P, V], F32, name=f"result{b}", align_bytes=64) for b in range(BLOCKS)]
+        total = [share.tile([P, 1], F32, name=f"total{b}", align_bytes=64, offset=EXCITE_AT + b * (ROW + LAP)) for b in range(2)]
+        total.extend(keep.tile([P, 1], F32, name=f"total{b}") for b in (2, 3))
         inverse = [keep.tile([P, 1], F32, name=f"inverse{b}") for b in range(BLOCKS)]
+
+        nc.vector.memset(xs[0:WIDE_AT, :].bitcast(I32), 0)
+        nc.vector.memset(es[0:WIDE_AT, :].bitcast(I32), 0)
+        nc.vector.memset(xs_plane[:].bitcast(I32), 0)
+        nc.vector.memset(es_plane[:].bitcast(I32), 0)
+        nc.vector.memset(mu_rows[:], 0.0)
+        nc.vector.memset(before_sb[:, 2:4, V : V + 1], 1.0)
+
+        def load_words(tile, words):
+            nc.sync.dma_start(tile[:].bitcast(I32), words[0].rearrange("p n j -> p (n j)").bitcast(I32))
+
+        def load_scales(tile, scales):
+            nc.scalar.dma_start(tile[WIDE_AT:P, :].bitcast(I32), scales[0].bitcast(I32))
+
+        def move_scales(plane, picked):
+            for r in range(QUADRANT_SCALES):
+                nc.sync.dma_start(plane[r:P:QUADRANT, :].bitcast(I32), picked[WIDE_AT + r : P : QUADRANT_SCALES, :].bitcast(I32))
+
+        def load_ago(b):
+            nc.sync.dma_start(ago_sb[b][:], ago[events(b), :])
+
+        def load_before(b):
+            nc.sync.dma_start(before_sb[:, b, 0:V], before[events(b), :])
 
         def gather(picked, table, offsets):
             nc.vector.tensor_copy(picked[:], table[:].indirect(offsets))
@@ -132,28 +133,29 @@ def tile_picked_yhawem_res_p_kernel(tc, x_words, x_scales, w1, e_words, e_scales
                     lhsT=w_codes[:, t * P : (t + 1) * P].bitcast(FP8X4),
                     lhsT_scale=w_scale[:, t * P : (t + 1) * P],
                     rhs=xw_picked[b // 2][:, in_half(b)].bitcast(FP8X4),
-                    rhs_scale=xs_picked[:, events(b)],
+                    rhs_scale=xs_plane[:, events(b)],
                     start=True,
                     stop=True,
                 )
 
         def relu(b):
             nc.scalar.activation(
-                h_bf[b // 2][:, in_half(b), :].rearrange("p (c i) t -> p c t i", i=4),
+                h_bf[:, events(b), :].rearrange("p (c i) t -> p c t i", i=4),
                 h_ps[b][:].rearrange("p t (c i) -> p c t i", i=4),
                 ACT.Relu,
             )
 
         def quantise_h(u):
-            nc.vector.quantize_mx(out=h_codes[u][:].bitcast(FP8X4), scales=h_scale[u][:], in_=h_bf[u][:].rearrange("p n t -> p (n t)"))
+            half = slice(u * HALF, (u + 1) * HALF)
+            nc.vector.quantize_mx(out=h_codes[:, half].bitcast(FP8X4), scales=h_scale[:, half], in_=h_bf[:, half, :].rearrange("p n t -> p (n t)"))
 
         def second_product(b):
             nc.tensor.matmul_mx(
                 y_ps[b][:],
-                lhsT=h_codes[b // 2][:, in_half(b)].bitcast(FP8X4),
-                lhsT_scale=h_scale[b // 2][:, in_half(b)],
+                lhsT=h_codes[:, events(b)].bitcast(FP8X4),
+                lhsT_scale=h_scale[:, events(b)],
                 rhs=ew_picked[:].bitcast(FP8X4),
-                rhs_scale=es_picked[E_SCALE_ROW:P, :],
+                rhs_scale=es_plane[:],
                 start=True,
                 stop=True,
             )
@@ -161,76 +163,100 @@ def tile_picked_yhawem_res_p_kernel(tc, x_words, x_scales, w1, e_words, e_scales
         def exp(b):
             nc.scalar.activation(decay[b][:], ago_sb[b][:], ACT.Exp, scale=DECAY_RATE)
 
-        def early_weight(b):
-            nc.vector.tensor_tensor(weight[b][:], decay[b][:], before_early[:, b, :], ALU.mult)
+        def excitation(b):
+            nc.vector.scalar_tensor_tensor(excite[b][:, 0:V], y_ps[b][:], 0.0, decay[b][:], ALU.max, ALU.mult)
 
-        def early_sum(b):
-            nc.vector.scalar_tensor_tensor(gg[b][:, 0:V], y_ps[b][:], 0.0, weight[b][:], ALU.max, ALU.mult, accum_out=total[b][:])
+        def masked_sum(b, width):
+            nc.vector.scalar_tensor_tensor(
+                gg[b][:, 0:width], excite[b][:, 0:width], 1.0, before_sb[:, b, 0:width], ALU.mult, ALU.mult, accum_out=total[b][:]
+            )
 
         def early_rate(b):
-            nc.vector.tensor_scalar(rate[b][:], total[b][:], mu_cols[:, MU_STEP * b : MU_STEP * b + 1], 1.0 / OUT_FACTOR, ALU.add, ALU.mult)
+            nc.scalar.activation(rate[b][:], total[b][:], ACT.Identity, bias=mu_part[:, b : b + 1], scale=1.0 / OUT_FACTOR)
 
-        def early_inverse(b):
-            nc.vector.reciprocal(inverse[b][:], rate[b][:])
+        def mu_column(b):
+            nc.scalar.copy(excite[b][:, V : V + 1], mu_cols[:, MU_STEP * b : MU_STEP * b + 1])
 
-        def early_result(b):
+        def invert(b, source):
+            nc.vector.reciprocal(inverse[b][:], source[:])
+
+        def scale_on_scalar(b):
             nc.scalar.activation(result[b][:], gg[b][:, 0:V], ACT.Copy, scale=inverse[b][:])
             nc.sync.dma_start(out[events(b), :], result[b][:])
 
-        def late_excite(b):
-            nc.vector.scalar_tensor_tensor(excite[b][:, 0:V], y_ps[b][:], 0.0, decay[b][:], ALU.max, ALU.mult)
+        def scale_piece(b, u):
+            cols = slice(u * HALF, (u + 1) * HALF)
+            nc.vector.tensor_scalar(result[b][:, cols], gg[b][:, cols], inverse[b][:], OUT_FACTOR, ALU.mult, ALU.mult)
+            nc.sync.dma_start(out[events(b), cols], result[b][:, cols])
 
-        def late_sum(b):
-            nc.vector.scalar_tensor_tensor(
-                gg[b][:, 0 : V + 1], excite[b][:, 0 : V + 1], 1.0, before_late[:, b - LATE[0], 0 : V + 1], ALU.mult, ALU.mult, accum_out=total[b][:]
-            )
-
-        def late_result(b):
+        def scale_on_vector(b):
             nc.vector.tensor_scalar(result[b][:], gg[b][:, 0:V], inverse[b][:], OUT_FACTOR, ALU.mult, ALU.mult)
             nc.sync.dma_start(out[events(b), :], result[b][:])
+
+        nc.sync.dma_start(offs_sb[:], offs)
+        load_scales(xs, x_scales)
+        nc.sync.dma_start(past_sb[:], past)
+        load_scales(es, e_scales)
+        nc.sync.dma_start(w_raw[:], w1.rearrange("(p j) c -> p j c", j=PACK))
+        nc.sync.dma_start(mu_rows[0:P:MU_STEP, :], mu.rearrange("(b q j) o -> q b (j o)", b=BLOCKS, q=P // QUADRANT))
+        load_words(xw, x_words)
+        gather(xs_picked, xs, offs_sb[:])
+        gather(es_picked, es, past_sb[:])
+        move_scales(xs_plane, xs_picked)
+        load_words(ew, e_words)
 
         w_src = w_raw[:].rearrange("p j (m t) -> p m j t", t=PACK)
         w_dst = w_bf[:].rearrange("p t m j -> p m j t")
         nc.vector.tensor_copy(w_dst[:, 0:CAST_VECTOR], w_src[:, 0:CAST_VECTOR])
         nc.scalar.copy(w_dst[:, CAST_VECTOR:P], w_src[:, CAST_VECTOR:P])
-        gather(xs_picked, xs, offs_sb[:])
+        move_scales(es_plane, es_picked)
+        load_ago(0)
+        load_before(0)
+        load_ago(1)
+        load_before(1)
+        load_ago(2)
+        load_ago(3)
+        nc.sync.dma_start(before_sb[:, 2:4, 0:V], before[2 * P : 4 * P, :].rearrange("(b p) v -> p b v", b=2))
+        nc.vector.transpose(mu_cols[:], mu_rows[:])
         nc.vector.quantize_mx(out=w_codes[:].bitcast(FP8X4), scales=w_scale[:], in_=w_bf[:].rearrange("p t m j -> p (t m j)"))
+        nc.scalar.activation(mu_part[:], mu_cols[:, 0 : 2 * MU_STEP : MU_STEP], ACT.Copy, scale=1.0 / OUT_FACTOR)
 
+        mu_column(2)
+        for b in range(2):
+            nc.tensor.matmul_mx(y_ps[b][:], lhsT=w_codes[:, 0:P].bitcast(FP8X4), lhsT_scale=w_scale[:, 0:P], rhs=w_codes[:].bitcast(FP8X4), rhs_scale=w_scale[:], start=True, stop=True)
         for u in range(2):
             gather(xw_picked[u], xw, offs_sb[:, u * HALF // LIST_ROWS : (u + 1) * HALF // LIST_ROWS])
         for b in range(BLOCKS):
             first_product(b)
+        nc.vector.tensor_scalar(h_bf[:, events(0), :], h_ps[0][:].rearrange("p t n -> p n t"), 0.0, None, ALU.max)
+        for b in range(1, BLOCKS):
             relu(b)
 
-        nc.vector.transpose(mu_cols[:], mu_rows[:])
-        nc.gpsimd.memset(before_late[:, :, V : V + 1], 1.0)
-        for b in LATE:
-            nc.gpsimd.tensor_copy(excite[b][:, V : V + 1], mu_cols[:, MU_STEP * b : MU_STEP * b + 1])
-
-        gather(es_picked, es, past_sb[:])
         gather(ew_picked, ew, past_sb[:])
         for u in range(2):
             quantise_h(u)
-        for b in range(BLOCKS):
+        for b in (1, 0, 2, 3):
             second_product(b)
-
         for b in range(BLOCKS):
             exp(b)
-        for b in EARLY:
-            early_weight(b)
-        for b in EARLY:
-            early_sum(b)
+        nc.vector.tensor_tensor(weight[:], decay[0][:], before_sb[:, 0, 0:V], ALU.mult)
+        excitation(1)
+        nc.vector.scalar_tensor_tensor(gg[0][:, 0:V], y_ps[0][:], 0.0, weight[:], ALU.max, ALU.mult, accum_out=total[0][:])
+        masked_sum(1, V)
         early_rate(0)
-        late_excite(2)
-        early_inverse(0)
+        nc.gpsimd.tensor_tensor(inverse[0][:], rate[0][:], minus_one[:], ALU.pow)
         early_rate(1)
-        early_result(0)
-        late_excite(3)
-        early_inverse(1)
-        early_result(1)
-        for b in LATE:
-            late_sum(b)
-        for b in LATE:
-            nc.vector.reciprocal(inverse[b][:], total[b][:])
-        for b in LATE:
-            late_result(b)
+        excitation(2)
+        invert(1, rate[1])
+        excitation(3)
+        mu_column(3)
+        for b in range(2):
+            scale_on_scalar(b)
+        masked_sum(2, V + 1)
+        invert(2, total[2])
+        masked_sum(3, V + 1)
+        scale_piece(2, 0)
+        invert(3, total[3])
+        scale_piece(2, 1)
+        for u in range(2):
+            scale_piece(3, u)

@@ -222,8 +222,6 @@ def tile_picked_yhawem_res_p_kernel(tc, x_words, x_scales, w1, e_words, e_scales
         nc.scalar.activation(mu_part[:], mu_cols[:, 0 : 2 * MU_STEP : MU_STEP], ACT.Copy, scale=1.0 / OUT_FACTOR)
 
         mu_column(2)
-        for b in range(2):
-            nc.tensor.matmul_mx(y_ps[b][:], lhsT=w_codes[:, 0:P].bitcast(FP8X4), lhsT_scale=w_scale[:, 0:P], rhs=w_codes[:].bitcast(FP8X4), rhs_scale=w_scale[:], start=True, stop=True)
         for u in range(2):
             gather(xw_picked[u], xw, offs_sb[:, u * HALF // LIST_ROWS : (u + 1) * HALF // LIST_ROWS])
         for b in range(BLOCKS):

@@ -30,15 +30,13 @@ FLOPS = 2 * K * H * S + 2 * H * S * V
 
 ROW = 4 * V
 LAP = 64
-XW_AT = 0
-EW_AT = XW_AT + 4 * T
-W_CODES_AT = EW_AT + 4 * T
+BANK = 2048
+W_CODES_AT = 0
 ES_AT = W_CODES_AT + 4 * H
-XW_PICKED_AT = ES_AT + T
-H_CODES_AT = XW_PICKED_AT + ROW
-ES_PICKED_AT = H_CODES_AT + 4 * S - LAP
-AGO_AT = ES_PICKED_AT + V
-EXCITE_AT = AGO_AT + BLOCKS * ROW
+ES_PICKED_AT = ES_AT + T
+AGO_AT = ES_PICKED_AT + 4 * HALF + 4 * P
+LAST_EXCITE_AT = AGO_AT + BLOCKS * ROW
+LAST_GG_AT = LAST_EXCITE_AT + ROW + LAP
 
 
 def tile_picked_yhawem_res_p_kernel(tc, x_words, x_scales, w1, e_words, e_scales, ago, before, mu, offs, past, out):
@@ -51,10 +49,13 @@ def tile_picked_yhawem_res_p_kernel(tc, x_words, x_scales, w1, e_words, e_scales
         def events(b):
             return slice(b * P, (b + 1) * P)
 
+        def half(u):
+            return slice(u * HALF, (u + 1) * HALF)
+
         offs_sb = keep.tile([P, S // LIST_ROWS], U16, name="offs_sb")
         past_sb = keep.tile([P, V // LIST_ROWS], U16, name="past_sb")
-        xw = share.tile([P, T], U32, name="xw", align_bytes=64, offset=XW_AT)
-        ew = share.tile([P, T], U32, name="ew", align_bytes=64, offset=EW_AT)
+        xw = keep.tile([P, T], U32, name="xw", align_bytes=64)
+        ew = keep.tile([P, T], U32, name="ew", align_bytes=64)
         xs = keep.tile([P, T], U8, name="xs", align_bytes=64)
         es = share.tile([P, T], U8, name="es", align_bytes=64, offset=ES_AT)
         w_raw = keep.tile([P, PACK, H], F32, name="w_raw", align_bytes=64)
@@ -63,46 +64,50 @@ def tile_picked_yhawem_res_p_kernel(tc, x_words, x_scales, w1, e_words, e_scales
         mu_rows = keep.tile([P, QUADRANT], F32, name="mu_rows", align_bytes=64)
         mu_cols = share.tile([P, QUADRANT], F32, name="mu_cols", align_bytes=64, offset=ES_AT)
         xs_picked = keep.tile([P, S], U8, name="xs_picked", align_bytes=64)
-        es_picked = share.tile([P, V], U8, name="es_picked", align_bytes=64, offset=ES_PICKED_AT)
+        es_picked = share.tile([P, V], U8, name="es_picked", align_bytes=64, offset=ES_PICKED_AT + 4 * HALF - LAP)
         xs_plane = keep.tile([P, S], U8, name="xs_plane", align_bytes=64)
         es_plane = keep.tile([P, V], U8, name="es_plane", align_bytes=64)
         ew_picked = keep.tile([P, V], U32, name="ew_picked", align_bytes=64)
-        xw_picked = [share.tile([P, HALF], U32, name=f"xw_picked{u}", align_bytes=64, offset=XW_PICKED_AT + 4 * HALF * u) for u in range(2)]
+        xw_picked = keep.tile([P, S], U32, name="xw_picked", align_bytes=64)
         w_bf = keep.tile([P, PACK, P, PACK], BF16, name="w_bf", align_bytes=64)
         w_codes = share.tile([P, H], U32, name="w_codes", align_bytes=64, offset=W_CODES_AT)
         w_scale = keep.tile([P, H], U8, name="w_scale", align_bytes=64)
-        h_ps = [psum.tile([P, PACK, P], F32, name=f"h_ps{b}") for b in range(BLOCKS)]
-        y_ps = [psum.tile([P, V], F32, name=f"y_ps{b}") for b in range(BLOCKS)]
-        h_bf = keep.tile([P, S, PACK], BF16, name="h_bf", align_bytes=64)
+        h_ps = [psum.tile([P, PACK, P], F32, name=f"h_ps{b}", offset=BANK * b) for b in range(BLOCKS)]
+        y_first = [psum.tile([P, HALF], F32, name=f"y_first{u}", offset=BANK * BLOCKS * (1 - u)) for u in range(2)]
+        y_ps = {b: psum.tile([P, V], F32, name=f"y_ps{b}", offset=BANK * (BLOCKS + b)) for b in range(1, BLOCKS)}
+        h_bf = [keep.tile([P, P, PACK], BF16, name=f"h_bf{b}", align_bytes=64) for b in range(BLOCKS - 1)]
+        h_bf.append(share.tile([P, P, PACK], BF16, name="h_bf3", align_bytes=64, offset=AGO_AT))
         h_scale = keep.tile([P, S], U8, name="h_scale", align_bytes=64)
-        h_codes = share.tile([P, S], U32, name="h_codes", align_bytes=64, offset=H_CODES_AT)
-        decay = [
-            share.tile([P, V], F32, name="decay0", align_bytes=64, offset=W_CODES_AT),
-            share.tile([P, V], F32, name="decay1", align_bytes=64, offset=XW_PICKED_AT),
-            keep.tile([P, V], F32, name="decay2", align_bytes=64),
-            keep.tile([P, V], F32, name="decay3", align_bytes=64),
+        h_codes = [
+            keep.tile([P, P], U32, name="h_codes0", align_bytes=64),
+            share.tile([P, P], U32, name="h_codes1", align_bytes=64, offset=ES_PICKED_AT + 4 * HALF),
+            share.tile([P, P], U32, name="h_codes2", align_bytes=64, offset=ES_PICKED_AT + 4 * P),
+            keep.tile([P, P], U32, name="h_codes3", align_bytes=64),
         ]
-        weight = keep.tile([P, V], F32, name="weight", align_bytes=64)
-        mu_part = keep.tile([P, 2], F32, name="mu_part")
-        rate = [share.tile([P, 1], F32, name=f"rate{b}", align_bytes=64, offset=AGO_AT + 3 * ROW + LAP * b) for b in range(2)]
-        excite = {1: keep.tile([P, V], F32, name="excite1", align_bytes=64)}
-        excite.setdefault(2, keep.tile([P, V + PAD], F32, name="excite2", align_bytes=64))
-        excite.setdefault(3, share.tile([P, V + PAD], F32, name="excite3", align_bytes=64, offset=EXCITE_AT + ROW + LAP))
-        minus_one = keep.tile([P, 1], F32, name="minus_one")
-        nc.gpsimd.memset(minus_one[:], -1.0)
-        gg = [share.tile([P, V], F32, name="gg0", align_bytes=64, offset=AGO_AT + ROW)]
-        gg.extend(keep.tile([P, V + PAD], F32, name=f"gg{b}", align_bytes=64) for b in range(1, BLOCKS))
-        result = [keep.tile([P, V], F32, name=f"result{b}", align_bytes=64) for b in range(BLOCKS)]
-        total = [share.tile([P, 1], F32, name=f"total{b}", align_bytes=64, offset=EXCITE_AT + b * (ROW + LAP)) for b in range(2)]
-        total.extend(keep.tile([P, 1], F32, name=f"total{b}") for b in (2, 3))
-        inverse = [keep.tile([P, 1], F32, name=f"inverse{b}") for b in range(BLOCKS)]
+        decay = [share.tile([P, V], F32, name="decay0", align_bytes=64, offset=W_CODES_AT)]
+        decay.extend(keep.tile([P, V], F32, name=f"decay{b}", align_bytes=64) for b in range(1, BLOCKS))
+        excite012 = keep.tile([P, BLOCKS - 1, V + PAD], F32, name="excite012", align_bytes=64)
+        excite3 = share.tile([P, V + PAD], F32, name="excite3", align_bytes=64, offset=LAST_EXCITE_AT)
+        excite = [excite012[:, 0, :], excite012[:, 1, :], excite012[:, 2, :], excite3[:]]
+        gg_rows = keep.tile([P, BLOCKS, V + PAD], F32, name="gg_rows", align_bytes=64)
+        gg_last = share.tile([P, HALF + PAD], F32, name="gg_last", align_bytes=64, offset=LAST_GG_AT)
+        total01 = share.tile([P, 2, PAD], F32, name="total01", align_bytes=64, offset=LAST_EXCITE_AT)
+        total2 = share.tile([P, 1], F32, name="total2", align_bytes=64, offset=LAST_GG_AT)
+        total3 = keep.tile([P, 1], F32, name="total3")
+        rate01 = share.tile([P, 2], F32, name="rate01", align_bytes=64, offset=AGO_AT + 2 * ROW)
+        rate2 = keep.tile([P, 1], F32, name="rate2")
+        inverse01 = keep.tile([P, 2], F32, name="inverse01")
+        inverse = [inverse01[:, 0:1], inverse01[:, 1:2]]
+        inverse.extend(keep.tile([P, 1], F32, name=f"inverse{b}")[:] for b in (2, 3))
+        result = [share.tile([P, V], F32, name="result0", align_bytes=64, offset=AGO_AT + 3 * ROW)]
+        result.extend(keep.tile([P, V], F32, name=f"result{b}", align_bytes=64) for b in range(1, BLOCKS))
 
         nc.vector.memset(xs[0:WIDE_AT, :].bitcast(I32), 0)
         nc.vector.memset(es[0:WIDE_AT, :].bitcast(I32), 0)
         nc.vector.memset(xs_plane[:].bitcast(I32), 0)
         nc.vector.memset(es_plane[:].bitcast(I32), 0)
         nc.vector.memset(mu_rows[:], 0.0)
-        nc.vector.memset(before_sb[:, 2:4, V : V + 1], 1.0)
+        nc.vector.memset(before_sb[:, :, V : V + 2], 1.0)
 
         def load_words(tile, words):
             nc.sync.dma_start(tile[:].bitcast(I32), words[0].rearrange("p n j -> p (n j)").bitcast(I32))
@@ -117,14 +122,11 @@ def tile_picked_yhawem_res_p_kernel(tc, x_words, x_scales, w1, e_words, e_scales
         def load_ago(b):
             nc.sync.dma_start(ago_sb[b][:], ago[events(b), :])
 
-        def load_before(b):
-            nc.sync.dma_start(before_sb[:, b, 0:V], before[events(b), :])
+        def load_before(u):
+            nc.sync.dma_start(before_sb[:, 2 * u : 2 * u + 2, 0:V], before[half(u), :].rearrange("(b p) v -> p b v", b=2))
 
-        def gather(picked, table, offsets):
-            nc.vector.tensor_copy(picked[:], table[:].indirect(offsets))
-
-        def in_half(b):
-            return slice((b % 2) * P, (b % 2 + 1) * P)
+        def gather(picked, table, offsets, first, last):
+            nc.vector.tensor_copy(picked[:, first:last], table[:].indirect(offsets[:, first // LIST_ROWS : last // LIST_ROWS]))
 
         def first_product(b):
             for t in range(PACK):
@@ -132,7 +134,7 @@ def tile_picked_yhawem_res_p_kernel(tc, x_words, x_scales, w1, e_words, e_scales
                     h_ps[b][:, t, :],
                     lhsT=w_codes[:, t * P : (t + 1) * P].bitcast(FP8X4),
                     lhsT_scale=w_scale[:, t * P : (t + 1) * P],
-                    rhs=xw_picked[b // 2][:, in_half(b)].bitcast(FP8X4),
+                    rhs=xw_picked[:, events(b)].bitcast(FP8X4),
                     rhs_scale=xs_plane[:, events(b)],
                     start=True,
                     stop=True,
@@ -140,22 +142,21 @@ def tile_picked_yhawem_res_p_kernel(tc, x_words, x_scales, w1, e_words, e_scales
 
         def relu(b):
             nc.scalar.activation(
-                h_bf[:, events(b), :].rearrange("p (c i) t -> p c t i", i=4),
+                h_bf[b][:].rearrange("p (c i) t -> p c t i", i=4),
                 h_ps[b][:].rearrange("p t (c i) -> p c t i", i=4),
                 ACT.Relu,
             )
 
-        def quantise_h(u):
-            half = slice(u * HALF, (u + 1) * HALF)
-            nc.vector.quantize_mx(out=h_codes[:, half].bitcast(FP8X4), scales=h_scale[:, half], in_=h_bf[:, half, :].rearrange("p n t -> p (n t)"))
+        def quantise_h(b):
+            nc.vector.quantize_mx(out=h_codes[b][:].bitcast(FP8X4), scales=h_scale[:, events(b)], in_=h_bf[b][:].rearrange("p n t -> p (n t)"))
 
-        def second_product(b):
+        def second_product(b, cols, y):
             nc.tensor.matmul_mx(
-                y_ps[b][:],
-                lhsT=h_codes[:, events(b)].bitcast(FP8X4),
+                y[:],
+                lhsT=h_codes[b][:].bitcast(FP8X4),
                 lhsT_scale=h_scale[:, events(b)],
-                rhs=ew_picked[:].bitcast(FP8X4),
-                rhs_scale=es_plane[:],
+                rhs=ew_picked[:, cols].bitcast(FP8X4),
+                rhs_scale=es_plane[:, cols],
                 start=True,
                 stop=True,
             )
@@ -163,35 +164,19 @@ def tile_picked_yhawem_res_p_kernel(tc, x_words, x_scales, w1, e_words, e_scales
         def exp(b):
             nc.scalar.activation(decay[b][:], ago_sb[b][:], ACT.Exp, scale=DECAY_RATE)
 
-        def excitation(b):
-            nc.vector.scalar_tensor_tensor(excite[b][:, 0:V], y_ps[b][:], 0.0, decay[b][:], ALU.max, ALU.mult)
+        def excitation(b, cols, y):
+            nc.vector.scalar_tensor_tensor(excite[b][:, cols], y[:], 0.0, decay[b][:, cols], ALU.max, ALU.mult)
 
-        def masked_sum(b, width):
-            nc.vector.scalar_tensor_tensor(
-                gg[b][:, 0:width], excite[b][:, 0:width], 1.0, before_sb[:, b, 0:width], ALU.mult, ALU.mult, accum_out=total[b][:]
-            )
+        def masked_sum(b, cols, gg, accum):
+            nc.vector.scalar_tensor_tensor(gg, excite[b][:, cols], 1.0, before_sb[:, b, cols], ALU.mult, ALU.mult, accum_out=accum)
 
-        def early_rate(b):
-            nc.scalar.activation(rate[b][:], total[b][:], ACT.Identity, bias=mu_part[:, b : b + 1], scale=1.0 / OUT_FACTOR)
-
-        def mu_column(b):
-            nc.scalar.copy(excite[b][:, V : V + 1], mu_cols[:, MU_STEP * b : MU_STEP * b + 1])
-
-        def invert(b, source):
-            nc.vector.reciprocal(inverse[b][:], source[:])
-
-        def scale_on_scalar(b):
-            nc.scalar.activation(result[b][:], gg[b][:, 0:V], ACT.Copy, scale=inverse[b][:])
-            nc.sync.dma_start(out[events(b), :], result[b][:])
-
-        def scale_piece(b, u):
-            cols = slice(u * HALF, (u + 1) * HALF)
-            nc.vector.tensor_scalar(result[b][:, cols], gg[b][:, cols], inverse[b][:], OUT_FACTOR, ALU.mult, ALU.mult)
+        def scale_on_scalar(b, cols):
+            nc.scalar.activation(result[b][:, cols], gg_rows[:, b, cols], ACT.Copy, scale=inverse[b])
             nc.sync.dma_start(out[events(b), cols], result[b][:, cols])
 
-        def scale_on_vector(b):
-            nc.vector.tensor_scalar(result[b][:], gg[b][:, 0:V], inverse[b][:], OUT_FACTOR, ALU.mult, ALU.mult)
-            nc.sync.dma_start(out[events(b), :], result[b][:])
+        def scale_on_vector(b, cols, gg):
+            nc.vector.tensor_scalar(result[b][:, cols], gg, inverse[b], OUT_FACTOR, ALU.mult, ALU.mult)
+            nc.sync.dma_start(out[events(b), cols], result[b][:, cols])
 
         nc.sync.dma_start(offs_sb[:], offs)
         load_scales(xs, x_scales)
@@ -200,8 +185,8 @@ def tile_picked_yhawem_res_p_kernel(tc, x_words, x_scales, w1, e_words, e_scales
         nc.sync.dma_start(w_raw[:], w1.rearrange("(p j) c -> p j c", j=PACK))
         nc.sync.dma_start(mu_rows[0:P:MU_STEP, :], mu.rearrange("(b q j) o -> q b (j o)", b=BLOCKS, q=P // QUADRANT))
         load_words(xw, x_words)
-        gather(xs_picked, xs, offs_sb[:])
-        gather(es_picked, es, past_sb[:])
+        gather(xs_picked, xs, offs_sb, 0, S)
+        gather(es_picked, es, past_sb, 0, V)
         move_scales(xs_plane, xs_picked)
         load_words(ew, e_words)
 
@@ -211,50 +196,55 @@ def tile_picked_yhawem_res_p_kernel(tc, x_words, x_scales, w1, e_words, e_scales
         nc.scalar.copy(w_dst[:, CAST_VECTOR:P], w_src[:, CAST_VECTOR:P])
         move_scales(es_plane, es_picked)
         load_ago(0)
-        load_before(0)
         load_ago(1)
-        load_before(1)
+        load_before(0)
         load_ago(2)
         load_ago(3)
-        nc.sync.dma_start(before_sb[:, 2:4, 0:V], before[2 * P : 4 * P, :].rearrange("(b p) v -> p b v", b=2))
+        load_before(1)
         nc.vector.transpose(mu_cols[:], mu_rows[:])
         nc.vector.quantize_mx(out=w_codes[:].bitcast(FP8X4), scales=w_scale[:], in_=w_bf[:].rearrange("p t m j -> p (t m j)"))
-        nc.scalar.activation(mu_part[:], mu_cols[:, 0 : 2 * MU_STEP : MU_STEP], ACT.Copy, scale=1.0 / OUT_FACTOR)
+        nc.scalar.copy(excite012[:, :, V], mu_cols[:, 0 : 3 * MU_STEP : MU_STEP])
 
-        mu_column(2)
-        for u in range(2):
-            gather(xw_picked[u], xw, offs_sb[:, u * HALF // LIST_ROWS : (u + 1) * HALF // LIST_ROWS])
+        for first, last in ((0, P), (P, HALF), (HALF, S)):
+            gather(xw_picked, xw, offs_sb, first, last)
         for b in range(BLOCKS):
             first_product(b)
-        nc.vector.tensor_scalar(h_bf[:, events(0), :], h_ps[0][:].rearrange("p t n -> p n t"), 0.0, None, ALU.max)
-        for b in range(1, BLOCKS):
+        for b in range(3):
             relu(b)
-
-        gather(ew_picked, ew, past_sb[:])
+        quantise_h(0)
         for u in range(2):
-            quantise_h(u)
-        for b in (1, 0, 2, 3):
-            second_product(b)
-        for b in range(BLOCKS):
-            exp(b)
-        nc.vector.tensor_tensor(weight[:], decay[0][:], before_sb[:, 0, 0:V], ALU.mult)
-        excitation(1)
-        nc.vector.scalar_tensor_tensor(gg[0][:, 0:V], y_ps[0][:], 0.0, weight[:], ALU.max, ALU.mult, accum_out=total[0][:])
-        masked_sum(1, V)
-        early_rate(0)
-        nc.gpsimd.tensor_tensor(inverse[0][:], rate[0][:], minus_one[:], ALU.pow)
-        early_rate(1)
-        excitation(2)
-        invert(1, rate[1])
-        excitation(3)
-        mu_column(3)
+            gather(ew_picked, ew, past_sb, u * HALF, (u + 1) * HALF)
+            second_product(0, half(u), y_first[u])
+        for b in (1, 2):
+            quantise_h(b)
+            second_product(b, slice(0, V), y_ps[b])
         for b in range(2):
-            scale_on_scalar(b)
-        masked_sum(2, V + 1)
-        invert(2, total[2])
-        masked_sum(3, V + 1)
-        scale_piece(2, 0)
-        invert(3, total[3])
-        scale_piece(2, 1)
+            exp(b)
+        relu(3)
+        exp(2)
         for u in range(2):
-            scale_piece(3, u)
+            excitation(0, half(u), y_first[u])
+        excitation(1, slice(0, V), y_ps[1])
+        quantise_h(3)
+        second_product(3, slice(0, V), y_ps[3])
+        for b in range(2):
+            masked_sum(b, slice(0, V + 1), gg_rows[:, b, 0 : V + 1], total01[:, b, 0:1])
+        excitation(2, slice(0, V), y_ps[2])
+        nc.scalar.activation(rate01[:], total01[:, :, 0], ACT.Copy, scale=1.0 / OUT_FACTOR)
+        nc.vector.reciprocal(inverse01[:], rate01[:])
+        exp(3)
+        excitation(3, slice(0, V), y_ps[3])
+        nc.scalar.copy(excite3[:, V : V + 1], mu_cols[:, 3 * MU_STEP : 3 * MU_STEP + 1])
+        for b in range(2):
+            scale_on_scalar(b, slice(0, V))
+        masked_sum(2, slice(0, V + 1), gg_rows[:, 2, 0 : V + 1], total2[:])
+        masked_sum(3, half(0), gg_rows[:, 3, half(0)], excite3[:, V + 1 : V + 2])
+        nc.scalar.activation(rate2[:], total2[:], ACT.Copy, scale=1.0 / OUT_FACTOR)
+        nc.vector.reciprocal(inverse[2], rate2[:])
+        masked_sum(3, slice(HALF, V + 2), gg_last[:, 0 : HALF + 2], total3[:])
+        scale_on_scalar(2, half(0))
+        nc.vector.tensor_scalar(result[2][:, half(1)], gg_rows[:, 2, half(1)], inverse[2], None, ALU.mult)
+        nc.sync.dma_start(out[events(2), half(1)], result[2][:, half(1)])
+        nc.vector.reciprocal(inverse[3], total3[:])
+        scale_on_vector(3, half(0), gg_rows[:, 3, half(0)])
+        scale_on_vector(3, half(1), gg_last[:, 0:HALF])

@@ -37,6 +37,7 @@ ES_PICKED_AT = ES_AT + T
 AGO_AT = ES_PICKED_AT + 4 * HALF + 4 * P
 LAST_EXCITE_AT = AGO_AT + BLOCKS * ROW
 LAST_GG_AT = LAST_EXCITE_AT + ROW + LAP
+BEFORE0_AT = LAST_GG_AT + ROW
 
 
 def tile_picked_yhawem_res_p_kernel(tc, x_words, x_scales, w1, e_words, e_scales, ago, before, mu, offs, past, out):
@@ -60,7 +61,8 @@ def tile_picked_yhawem_res_p_kernel(tc, x_words, x_scales, w1, e_words, e_scales
         es = share.tile([P, T], U8, name="es", align_bytes=64, offset=ES_AT)
         w_raw = keep.tile([P, PACK, H], F32, name="w_raw", align_bytes=64)
         ago_sb = [share.tile([P, V], F32, name=f"ago{b}", align_bytes=64, offset=AGO_AT + ROW * b) for b in range(BLOCKS)]
-        before_sb = keep.tile([P, BLOCKS, V + PAD], F32, name="before_sb", align_bytes=64)
+        before01 = [share.tile([P, V], F32, name="before0", align_bytes=64, offset=BEFORE0_AT), keep.tile([P, V], F32, name="before1", align_bytes=64)]
+        before23 = keep.tile([P, 2, V + PAD], F32, name="before23", align_bytes=64)
         mu_rows = keep.tile([P, QUADRANT], F32, name="mu_rows", align_bytes=64)
         mu_cols = share.tile([P, QUADRANT], F32, name="mu_cols", align_bytes=64, offset=ES_AT)
         xs_picked = keep.tile([P, S], U8, name="xs_picked", align_bytes=64)
@@ -75,17 +77,15 @@ def tile_picked_yhawem_res_p_kernel(tc, x_words, x_scales, w1, e_words, e_scales
         h_ps = [psum.tile([P, PACK, P], F32, name=f"h_ps{b}", offset=BANK * b) for b in range(BLOCKS)]
         y_first = [psum.tile([P, HALF], F32, name=f"y_first{u}", offset=BANK * BLOCKS * (1 - u)) for u in range(2)]
         y_ps = {b: psum.tile([P, V], F32, name=f"y_ps{b}", offset=BANK * (BLOCKS + b)) for b in range(1, BLOCKS)}
-        h_bf = [keep.tile([P, P, PACK], BF16, name=f"h_bf{b}", align_bytes=64) for b in range(BLOCKS - 1)]
-        h_bf.append(share.tile([P, P, PACK], BF16, name="h_bf3", align_bytes=64, offset=AGO_AT))
+        h_bf = [keep.tile([P, P, PACK], BF16, name=f"h_bf{b}", align_bytes=64) for b in range(BLOCKS)]
         h_scale = keep.tile([P, S], U8, name="h_scale", align_bytes=64)
         h_codes = [
             keep.tile([P, P], U32, name="h_codes0", align_bytes=64),
             share.tile([P, P], U32, name="h_codes1", align_bytes=64, offset=ES_PICKED_AT + 4 * HALF),
             share.tile([P, P], U32, name="h_codes2", align_bytes=64, offset=ES_PICKED_AT + 4 * P),
-            keep.tile([P, P], U32, name="h_codes3", align_bytes=64),
+            share.tile([P, P], U32, name="h_codes3", align_bytes=64, offset=BEFORE0_AT),
         ]
-        decay = [share.tile([P, V], F32, name="decay0", align_bytes=64, offset=W_CODES_AT)]
-        decay.extend(keep.tile([P, V], F32, name=f"decay{b}", align_bytes=64) for b in range(1, BLOCKS))
+        decay = [keep.tile([P, V + PAD], F32, name=f"decay{b}", align_bytes=64) for b in range(BLOCKS)]
         excite012 = keep.tile([P, BLOCKS - 1, V + PAD], F32, name="excite012", align_bytes=64)
         excite3 = share.tile([P, V + PAD], F32, name="excite3", align_bytes=64, offset=LAST_EXCITE_AT)
         excite = [excite012[:, 0, :], excite012[:, 1, :], excite012[:, 2, :], excite3[:]]
@@ -107,10 +107,12 @@ def tile_picked_yhawem_res_p_kernel(tc, x_words, x_scales, w1, e_words, e_scales
         nc.vector.memset(xs_plane[:].bitcast(I32), 0)
         nc.vector.memset(es_plane[:].bitcast(I32), 0)
         nc.vector.memset(mu_rows[:], 0.0)
-        nc.vector.memset(before_sb[:, :, V : V + 2], 1.0)
+        nc.vector.memset(before23[:, :, V : V + 2], 1.0)
+        for b in range(2):
+            nc.vector.memset(decay[b][:, V : V + 1], 1.0)
 
-        def load_words(tile, words):
-            nc.sync.dma_start(tile[:].bitcast(I32), words[0].rearrange("p n j -> p (n j)").bitcast(I32))
+        def load_words(tile, words, first, last):
+            nc.sync.dma_start(tile[:, first:last].bitcast(I32), words[0].rearrange("p n j -> p (n j)").bitcast(I32)[:, first:last])
 
         def load_scales(tile, scales):
             nc.scalar.dma_start(tile[WIDE_AT:P, :].bitcast(I32), scales[0].bitcast(I32))
@@ -122,8 +124,8 @@ def tile_picked_yhawem_res_p_kernel(tc, x_words, x_scales, w1, e_words, e_scales
         def load_ago(b):
             nc.sync.dma_start(ago_sb[b][:], ago[events(b), :])
 
-        def load_before(u):
-            nc.sync.dma_start(before_sb[:, 2 * u : 2 * u + 2, 0:V], before[half(u), :].rearrange("(b p) v -> p b v", b=2))
+        def load_before(b):
+            nc.sync.dma_start(before01[b][:], before[events(b), :])
 
         def gather(picked, table, offsets, first, last):
             nc.vector.tensor_copy(picked[:, first:last], table[:].indirect(offsets[:, first // LIST_ROWS : last // LIST_ROWS]))
@@ -162,13 +164,15 @@ def tile_picked_yhawem_res_p_kernel(tc, x_words, x_scales, w1, e_words, e_scales
             )
 
         def exp(b):
-            nc.scalar.activation(decay[b][:], ago_sb[b][:], ACT.Exp, scale=DECAY_RATE)
+            nc.scalar.activation(decay[b][:, 0:V], ago_sb[b][:], ACT.Exp, scale=DECAY_RATE)
 
         def excitation(b, cols, y):
-            nc.vector.scalar_tensor_tensor(excite[b][:, cols], y[:], 0.0, decay[b][:, cols], ALU.max, ALU.mult)
+            factor = before01[b][:, cols] if b < 2 else decay[b][:, cols]
+            nc.vector.scalar_tensor_tensor(excite[b][:, cols], y[:], 0.0, factor, ALU.max, ALU.mult)
 
         def masked_sum(b, cols, gg, accum):
-            nc.vector.scalar_tensor_tensor(gg, excite[b][:, cols], 1.0, before_sb[:, b, cols], ALU.mult, ALU.mult, accum_out=accum)
+            factor = decay[b][:, cols] if b < 2 else before23[:, b - 2, cols]
+            nc.vector.scalar_tensor_tensor(gg, excite[b][:, cols], 1.0, factor, ALU.mult, ALU.mult, accum_out=accum)
 
         def scale_on_scalar(b, cols):
             nc.scalar.activation(result[b][:, cols], gg_rows[:, b, cols], ACT.Copy, scale=inverse[b])
@@ -184,23 +188,23 @@ def tile_picked_yhawem_res_p_kernel(tc, x_words, x_scales, w1, e_words, e_scales
         load_scales(es, e_scales)
         nc.sync.dma_start(w_raw[:], w1.rearrange("(p j) c -> p j c", j=PACK))
         nc.sync.dma_start(mu_rows[0:P:MU_STEP, :], mu.rearrange("(b q j) o -> q b (j o)", b=BLOCKS, q=P // QUADRANT))
-        load_words(xw, x_words)
+        load_words(xw, x_words, 0, 3 * T // 4)
         gather(xs_picked, xs, offs_sb, 0, S)
         gather(es_picked, es, past_sb, 0, V)
         move_scales(xs_plane, xs_picked)
-        load_words(ew, e_words)
+        load_words(xw, x_words, 3 * T // 4, T)
+        load_words(ew, e_words, 0, T)
 
         w_src = w_raw[:].rearrange("p j (m t) -> p m j t", t=PACK)
         w_dst = w_bf[:].rearrange("p t m j -> p m j t")
         nc.vector.tensor_copy(w_dst[:, 0:CAST_VECTOR], w_src[:, 0:CAST_VECTOR])
         nc.scalar.copy(w_dst[:, CAST_VECTOR:P], w_src[:, CAST_VECTOR:P])
         move_scales(es_plane, es_picked)
-        load_ago(0)
-        load_ago(1)
-        load_before(0)
-        load_ago(2)
-        load_ago(3)
-        load_before(1)
+        for b in range(2):
+            load_before(b)
+        for b in range(BLOCKS):
+            load_ago(b)
+        nc.sync.dma_start(before23[:, :, 0:V], before[half(1), :].rearrange("(b p) v -> p b v", b=2))
         nc.vector.transpose(mu_cols[:], mu_rows[:])
         nc.vector.quantize_mx(out=w_codes[:].bitcast(FP8X4), scales=w_scale[:], in_=w_bf[:].rearrange("p t m j -> p (t m j)"))
         nc.scalar.copy(excite012[:, :, V], mu_cols[:, 0 : 3 * MU_STEP : MU_STEP])
@@ -209,7 +213,7 @@ def tile_picked_yhawem_res_p_kernel(tc, x_words, x_scales, w1, e_words, e_scales
             gather(xw_picked, xw, offs_sb, first, last)
         for b in range(BLOCKS):
             first_product(b)
-        for b in range(3):
+        for b in range(BLOCKS):
             relu(b)
         quantise_h(0)
         for u in range(2):
@@ -218,10 +222,8 @@ def tile_picked_yhawem_res_p_kernel(tc, x_words, x_scales, w1, e_words, e_scales
         for b in (1, 2):
             quantise_h(b)
             second_product(b, slice(0, V), y_ps[b])
-        for b in range(2):
+        for b in range(3):
             exp(b)
-        relu(3)
-        exp(2)
         for u in range(2):
             excitation(0, half(u), y_first[u])
         excitation(1, slice(0, V), y_ps[1])

@@ -35,7 +35,7 @@ W_CODES_AT = 0
 ES_AT = W_CODES_AT + 4 * H
 ES_PICKED_AT = ES_AT + T
 AGO_AT = ES_PICKED_AT + 4 * HALF + 4 * P
-LAST_EXCITE_AT = AGO_AT + BLOCKS * ROW
+LAST_EXCITE_AT = AGO_AT + BLOCKS * ROW + 2 * LAP
 LAST_GG_AT = LAST_EXCITE_AT + ROW + LAP
 BEFORE0_AT = LAST_GG_AT + ROW
 
@@ -60,7 +60,7 @@ def tile_picked_yhawem_res_p_kernel(tc, x_words, x_scales, w1, e_words, e_scales
         xs = keep.tile([P, T], U8, name="xs", align_bytes=64)
         es = share.tile([P, T], U8, name="es", align_bytes=64, offset=ES_AT)
         w_raw = keep.tile([P, PACK, H], F32, name="w_raw", align_bytes=64)
-        ago_sb = [share.tile([P, V], F32, name=f"ago{b}", align_bytes=64, offset=AGO_AT + ROW * b) for b in range(BLOCKS)]
+        ago_sb = [share.tile([P, V + (LAP // 2 if b == 3 else 0)], F32, name=f"ago{b}", align_bytes=64, offset=AGO_AT + ROW * b) for b in range(BLOCKS)]
         before01 = [share.tile([P, V], F32, name="before0", align_bytes=64, offset=BEFORE0_AT), keep.tile([P, V], F32, name="before1", align_bytes=64)]
         before23 = keep.tile([P, 2, V + PAD], F32, name="before23", align_bytes=64)
         mu_rows = keep.tile([P, QUADRANT], F32, name="mu_rows", align_bytes=64)
@@ -75,8 +75,8 @@ def tile_picked_yhawem_res_p_kernel(tc, x_words, x_scales, w1, e_words, e_scales
         w_codes = share.tile([P, H], U32, name="w_codes", align_bytes=64, offset=W_CODES_AT)
         w_scale = keep.tile([P, H], U8, name="w_scale", align_bytes=64)
         h_ps = [psum.tile([P, PACK, P], F32, name=f"h_ps{b}", offset=BANK * b) for b in range(BLOCKS)]
-        y_first = [psum.tile([P, HALF], F32, name=f"y_first{u}", offset=BANK * BLOCKS * (1 - u)) for u in range(2)]
-        y_ps = {b: psum.tile([P, V], F32, name=f"y_ps{b}", offset=BANK * (BLOCKS + b)) for b in range(1, BLOCKS)}
+        y_half = [[psum.tile([P, HALF], F32, name=f"y_half{b}{u}", offset=BANK * (b + BLOCKS * (1 - u))) for u in range(2)] for b in range(2)]
+        y_ps = {b: psum.tile([P, V], F32, name=f"y_ps{b}", offset=BANK * (BLOCKS + b)) for b in range(2, BLOCKS)}
         h_bf = [keep.tile([P, P, PACK], BF16, name=f"h_bf{b}", align_bytes=64) for b in range(BLOCKS)]
         h_scale = keep.tile([P, S], U8, name="h_scale", align_bytes=64)
         h_codes = [
@@ -91,14 +91,15 @@ def tile_picked_yhawem_res_p_kernel(tc, x_words, x_scales, w1, e_words, e_scales
         excite = [excite012[:, 0, :], excite012[:, 1, :], excite012[:, 2, :], excite3[:]]
         gg_rows = keep.tile([P, BLOCKS, V + PAD], F32, name="gg_rows", align_bytes=64)
         gg_last = share.tile([P, HALF + PAD], F32, name="gg_last", align_bytes=64, offset=LAST_GG_AT)
-        total01 = share.tile([P, 2, PAD], F32, name="total01", align_bytes=64, offset=LAST_EXCITE_AT)
+        total0 = keep.tile([P, 1], F32, name="total0")
+        total1 = keep.tile([P, 1], F32, name="total1")
+        plain_inverse0 = share.tile([P, 1], F32, name="plain_inverse0", align_bytes=64, offset=AGO_AT + ROW)
         total2 = share.tile([P, 1], F32, name="total2", align_bytes=64, offset=LAST_GG_AT)
         total3 = keep.tile([P, 1], F32, name="total3")
-        rate01 = share.tile([P, 2], F32, name="rate01", align_bytes=64, offset=AGO_AT + 2 * ROW)
+        rate1 = share.tile([P, 1], F32, name="rate1", align_bytes=64, offset=AGO_AT + BLOCKS * ROW + LAP)
         rate2 = keep.tile([P, 1], F32, name="rate2")
-        inverse01 = keep.tile([P, 2], F32, name="inverse01")
-        inverse = [inverse01[:, 0:1], inverse01[:, 1:2]]
-        inverse.extend(keep.tile([P, 1], F32, name=f"inverse{b}")[:] for b in (2, 3))
+        inverse = [share.tile([P, 1], F32, name="inverse0", align_bytes=64, offset=AGO_AT + BLOCKS * ROW)[:]]
+        inverse.extend(keep.tile([P, 1], F32, name=f"inverse{b}")[:] for b in (1, 2, 3))
         result = [share.tile([P, V], F32, name="result0", align_bytes=64, offset=AGO_AT + 3 * ROW)]
         result.extend(keep.tile([P, V], F32, name=f"result{b}", align_bytes=64) for b in range(1, BLOCKS))
 
@@ -122,7 +123,7 @@ def tile_picked_yhawem_res_p_kernel(tc, x_words, x_scales, w1, e_words, e_scales
                 nc.sync.dma_start(plane[r:P:QUADRANT, :].bitcast(I32), picked[WIDE_AT + r : P : QUADRANT_SCALES, :].bitcast(I32))
 
         def load_ago(b):
-            nc.sync.dma_start(ago_sb[b][:], ago[events(b), :])
+            nc.sync.dma_start(ago_sb[b][:, 0:V], ago[events(b), :])
 
         def load_before(b):
             nc.sync.dma_start(before01[b][:], before[events(b), :])
@@ -164,7 +165,7 @@ def tile_picked_yhawem_res_p_kernel(tc, x_words, x_scales, w1, e_words, e_scales
             )
 
         def exp(b):
-            nc.scalar.activation(decay[b][:, 0:V], ago_sb[b][:], ACT.Exp, scale=DECAY_RATE)
+            nc.scalar.activation(decay[b][:, 0:V], ago_sb[b][:, 0:V], ACT.Exp, scale=DECAY_RATE)
 
         def excitation(b, cols, y):
             factor = before01[b][:, cols] if b < 2 else decay[b][:, cols]
@@ -188,11 +189,10 @@ def tile_picked_yhawem_res_p_kernel(tc, x_words, x_scales, w1, e_words, e_scales
         load_scales(es, e_scales)
         nc.sync.dma_start(w_raw[:], w1.rearrange("(p j) c -> p j c", j=PACK))
         nc.sync.dma_start(mu_rows[0:P:MU_STEP, :], mu.rearrange("(b q j) o -> q b (j o)", b=BLOCKS, q=P // QUADRANT))
-        load_words(xw, x_words, 0, 3 * T // 4)
+        load_words(xw, x_words, 0, T)
         gather(xs_picked, xs, offs_sb, 0, S)
         gather(es_picked, es, past_sb, 0, V)
         move_scales(xs_plane, xs_picked)
-        load_words(xw, x_words, 3 * T // 4, T)
         load_words(ew, e_words, 0, T)
 
         w_src = w_raw[:].rearrange("p j (m t) -> p m j t", t=PACK)
@@ -218,24 +218,28 @@ def tile_picked_yhawem_res_p_kernel(tc, x_words, x_scales, w1, e_words, e_scales
         quantise_h(0)
         for u in range(2):
             gather(ew_picked, ew, past_sb, u * HALF, (u + 1) * HALF)
-            second_product(0, half(u), y_first[u])
-        for b in (1, 2):
-            quantise_h(b)
-            second_product(b, slice(0, V), y_ps[b])
+            second_product(0, half(u), y_half[0][u])
+        quantise_h(1)
+        for u in range(2):
+            second_product(1, half(u), y_half[1][u])
+        quantise_h(2)
+        second_product(2, slice(0, V), y_ps[2])
         for b in range(3):
             exp(b)
-        for u in range(2):
-            excitation(0, half(u), y_first[u])
-        excitation(1, slice(0, V), y_ps[1])
+        for b in range(2):
+            for u in range(2):
+                excitation(b, half(u), y_half[b][u])
         quantise_h(3)
         second_product(3, slice(0, V), y_ps[3])
-        for b in range(2):
-            masked_sum(b, slice(0, V + 1), gg_rows[:, b, 0 : V + 1], total01[:, b, 0:1])
+        masked_sum(0, slice(0, V + 1), gg_rows[:, 0, 0 : V + 1], total0[:])
+        masked_sum(1, slice(0, V + 1), gg_rows[:, 1, 0 : V + 1], total1[:])
+        nc.vector.reciprocal(plain_inverse0[:], total0[:])
         excitation(2, slice(0, V), y_ps[2])
-        nc.scalar.activation(rate01[:], total01[:, :, 0], ACT.Copy, scale=1.0 / OUT_FACTOR)
-        nc.vector.reciprocal(inverse01[:], rate01[:])
         exp(3)
+        nc.scalar.activation(inverse[0], plain_inverse0[:], ACT.Copy, scale=OUT_FACTOR)
+        nc.scalar.activation(rate1[:], total1[:], ACT.Copy, scale=1.0 / OUT_FACTOR)
         excitation(3, slice(0, V), y_ps[3])
+        nc.vector.reciprocal(inverse[1], rate1[:])
         nc.scalar.copy(excite3[:, V : V + 1], mu_cols[:, 3 * MU_STEP : 3 * MU_STEP + 1])
         for b in range(2):
             scale_on_scalar(b, slice(0, V))

@@ -37,7 +37,6 @@ ES_PICKED_AT = ES_AT + T
 AGO_AT = ES_PICKED_AT + 4 * HALF + 4 * P
 LAST_EXCITE_AT = AGO_AT + BLOCKS * ROW + 2 * LAP
 LAST_GG_AT = LAST_EXCITE_AT + ROW + LAP
-BEFORE0_AT = LAST_GG_AT + ROW
 
 
 def tile_picked_yhawem_res_p_kernel(tc, x_words, x_scales, w1, e_words, e_scales, ago, before, mu, offs, past, out):
@@ -61,7 +60,7 @@ def tile_picked_yhawem_res_p_kernel(tc, x_words, x_scales, w1, e_words, e_scales
         es = share.tile([P, T], U8, name="es", align_bytes=64, offset=ES_AT)
         w_raw = keep.tile([P, PACK, H], F32, name="w_raw", align_bytes=64)
         ago_sb = [share.tile([P, V + (LAP // 2 if b == 3 else 0)], F32, name=f"ago{b}", align_bytes=64, offset=AGO_AT + ROW * b) for b in range(BLOCKS)]
-        before01 = [share.tile([P, V], F32, name="before0", align_bytes=64, offset=BEFORE0_AT), keep.tile([P, V], F32, name="before1", align_bytes=64)]
+        before01 = keep.tile([P, 2, V], F32, name="before01", align_bytes=64)
         before23 = keep.tile([P, 2, V + PAD], F32, name="before23", align_bytes=64)
         mu_rows = keep.tile([P, QUADRANT], F32, name="mu_rows", align_bytes=64)
         mu_cols = share.tile([P, QUADRANT], F32, name="mu_cols", align_bytes=64, offset=ES_AT)
@@ -79,12 +78,9 @@ def tile_picked_yhawem_res_p_kernel(tc, x_words, x_scales, w1, e_words, e_scales
         y_ps = {b: psum.tile([P, V], F32, name=f"y_ps{b}", offset=BANK * (BLOCKS + b)) for b in range(2, BLOCKS)}
         h_bf = [keep.tile([P, P, PACK], BF16, name=f"h_bf{b}", align_bytes=64) for b in range(BLOCKS)]
         h_scale = keep.tile([P, S], U8, name="h_scale", align_bytes=64)
-        h_codes = [
-            keep.tile([P, P], U32, name="h_codes0", align_bytes=64),
-            share.tile([P, P], U32, name="h_codes1", align_bytes=64, offset=ES_PICKED_AT + 4 * HALF),
-            share.tile([P, P], U32, name="h_codes2", align_bytes=64, offset=ES_PICKED_AT + 4 * P),
-            share.tile([P, P], U32, name="h_codes3", align_bytes=64, offset=BEFORE0_AT),
-        ]
+        h_codes_late = share.tile([P, BLOCKS - 1, P], U32, name="h_codes_late", align_bytes=64, offset=ES_PICKED_AT)
+        h_codes = [keep.tile([P, P], U32, name="h_codes0", align_bytes=64)[:]]
+        h_codes.extend(h_codes_late[:, b, :] for b in range(BLOCKS - 1))
         decay = [keep.tile([P, V + PAD], F32, name=f"decay{b}", align_bytes=64) for b in range(BLOCKS)]
         excite012 = keep.tile([P, BLOCKS - 1, V + PAD], F32, name="excite012", align_bytes=64)
         excite3 = share.tile([P, V + PAD], F32, name="excite3", align_bytes=64, offset=LAST_EXCITE_AT)
@@ -125,9 +121,6 @@ def tile_picked_yhawem_res_p_kernel(tc, x_words, x_scales, w1, e_words, e_scales
         def load_ago(b):
             nc.sync.dma_start(ago_sb[b][:, 0:V], ago[events(b), :])
 
-        def load_before(b):
-            nc.sync.dma_start(before01[b][:], before[events(b), :])
-
         def gather(picked, table, offsets, first, last):
             nc.vector.tensor_copy(picked[:, first:last], table[:].indirect(offsets[:, first // LIST_ROWS : last // LIST_ROWS]))
 
@@ -151,12 +144,12 @@ def tile_picked_yhawem_res_p_kernel(tc, x_words, x_scales, w1, e_words, e_scales
             )
 
         def quantise_h(b):
-            nc.vector.quantize_mx(out=h_codes[b][:].bitcast(FP8X4), scales=h_scale[:, events(b)], in_=h_bf[b][:].rearrange("p n t -> p (n t)"))
+            nc.vector.quantize_mx(out=h_codes[b].bitcast(FP8X4), scales=h_scale[:, events(b)], in_=h_bf[b][:].rearrange("p n t -> p (n t)"))
 
         def second_product(b, cols, y):
             nc.tensor.matmul_mx(
                 y[:],
-                lhsT=h_codes[b][:].bitcast(FP8X4),
+                lhsT=h_codes[b].bitcast(FP8X4),
                 lhsT_scale=h_scale[:, events(b)],
                 rhs=ew_picked[:, cols].bitcast(FP8X4),
                 rhs_scale=es_plane[:, cols],
@@ -168,7 +161,7 @@ def tile_picked_yhawem_res_p_kernel(tc, x_words, x_scales, w1, e_words, e_scales
             nc.scalar.activation(decay[b][:, 0:V], ago_sb[b][:, 0:V], ACT.Exp, scale=DECAY_RATE)
 
         def excitation(b, cols, y):
-            factor = before01[b][:, cols] if b < 2 else decay[b][:, cols]
+            factor = before01[:, b, cols] if b < 2 else decay[b][:, cols]
             nc.vector.scalar_tensor_tensor(excite[b][:, cols], y[:], 0.0, factor, ALU.max, ALU.mult)
 
         def masked_sum(b, cols, gg, accum):
@@ -200,8 +193,7 @@ def tile_picked_yhawem_res_p_kernel(tc, x_words, x_scales, w1, e_words, e_scales
         nc.vector.tensor_copy(w_dst[:, 0:CAST_VECTOR], w_src[:, 0:CAST_VECTOR])
         nc.scalar.copy(w_dst[:, CAST_VECTOR:P], w_src[:, CAST_VECTOR:P])
         move_scales(es_plane, es_picked)
-        for b in range(2):
-            load_before(b)
+        nc.sync.dma_start(before01[:], before[half(0), :].rearrange("(b p) v -> p b v", b=2))
         for b in range(BLOCKS):
             load_ago(b)
         nc.sync.dma_start(before23[:, :, 0:V], before[half(1), :].rearrange("(b p) v -> p b v", b=2))
@@ -222,15 +214,14 @@ def tile_picked_yhawem_res_p_kernel(tc, x_words, x_scales, w1, e_words, e_scales
         quantise_h(1)
         for u in range(2):
             second_product(1, half(u), y_half[1][u])
-        quantise_h(2)
-        second_product(2, slice(0, V), y_ps[2])
+        for b in range(2, BLOCKS):
+            quantise_h(b)
+            second_product(b, slice(0, V), y_ps[b])
         for b in range(3):
             exp(b)
         for b in range(2):
             for u in range(2):
                 excitation(b, half(u), y_half[b][u])
-        quantise_h(3)
-        second_product(3, slice(0, V), y_ps[3])
         masked_sum(0, slice(0, V + 1), gg_rows[:, 0, 0 : V + 1], total0[:])
         masked_sum(1, slice(0, V + 1), gg_rows[:, 1, 0 : V + 1], total1[:])
         nc.vector.reciprocal(plain_inverse0[:], total0[:])

@@ -74,8 +74,8 @@ def tile_picked_yhawem_res_p_kernel(tc, x_words, x_scales, w1, e_words, e_scales
         w_codes = share.tile([P, H], U32, name="w_codes", align_bytes=64, offset=W_CODES_AT)
         w_scale = keep.tile([P, H], U8, name="w_scale", align_bytes=64)
         h_ps = [psum.tile([P, PACK, P], F32, name=f"h_ps{b}", offset=BANK * b) for b in range(BLOCKS)]
-        y_half = [[psum.tile([P, HALF], F32, name=f"y_half{b}{u}", offset=BANK * (b + BLOCKS * (1 - u))) for u in range(2)] for b in range(2)]
-        y_ps = {b: psum.tile([P, V], F32, name=f"y_ps{b}", offset=BANK * (BLOCKS + b)) for b in range(2, BLOCKS)}
+        y_half = [psum.tile([P, HALF], F32, name=f"y_half{u}", offset=BANK * BLOCKS * (1 - u)) for u in range(2)]
+        y_ps = {b: psum.tile([P, V], F32, name=f"y_ps{b}", offset=BANK * (BLOCKS + b)) for b in range(1, BLOCKS)}
         h_bf = [keep.tile([P, P, PACK], BF16, name=f"h_bf{b}", align_bytes=64) for b in range(BLOCKS)]
         h_scale = keep.tile([P, S], U8, name="h_scale", align_bytes=64)
         h_codes_late = share.tile([P, BLOCKS - 1, P], U32, name="h_codes_late", align_bytes=64, offset=ES_PICKED_AT)
@@ -92,10 +92,11 @@ def tile_picked_yhawem_res_p_kernel(tc, x_words, x_scales, w1, e_words, e_scales
         plain_inverse0 = share.tile([P, 1], F32, name="plain_inverse0", align_bytes=64, offset=AGO_AT + ROW)
         total2 = share.tile([P, 1], F32, name="total2", align_bytes=64, offset=LAST_GG_AT)
         total3 = keep.tile([P, 1], F32, name="total3")
-        rate1 = share.tile([P, 1], F32, name="rate1", align_bytes=64, offset=AGO_AT + BLOCKS * ROW + LAP)
+        plain_inverse1 = share.tile([P, 1], F32, name="plain_inverse1", align_bytes=64, offset=AGO_AT + 2 * ROW)
         rate2 = keep.tile([P, 1], F32, name="rate2")
         inverse = [share.tile([P, 1], F32, name="inverse0", align_bytes=64, offset=AGO_AT + BLOCKS * ROW)[:]]
-        inverse.extend(keep.tile([P, 1], F32, name=f"inverse{b}")[:] for b in (1, 2, 3))
+        inverse.append(share.tile([P, 1], F32, name="inverse1", align_bytes=64, offset=AGO_AT + BLOCKS * ROW + LAP)[:])
+        inverse.extend(keep.tile([P, 1], F32, name=f"inverse{b}")[:] for b in (2, 3))
         result = [share.tile([P, V], F32, name="result0", align_bytes=64, offset=AGO_AT + 3 * ROW)]
         result.extend(keep.tile([P, V], F32, name=f"result{b}", align_bytes=64) for b in range(1, BLOCKS))
 
@@ -157,12 +158,12 @@ def tile_picked_yhawem_res_p_kernel(tc, x_words, x_scales, w1, e_words, e_scales
                 stop=True,
             )
 
-        def exp(b):
-            nc.scalar.activation(decay[b][:, 0:V], ago_sb[b][:, 0:V], ACT.Exp, scale=DECAY_RATE)
+        def exp(b, cols):
+            nc.scalar.activation(decay[b][:, cols], ago_sb[b][:, cols], ACT.Exp, scale=DECAY_RATE)
 
         def excitation(b, cols, y):
             factor = before01[:, b, cols] if b < 2 else decay[b][:, cols]
-            nc.vector.scalar_tensor_tensor(excite[b][:, cols], y[:], 0.0, factor, ALU.max, ALU.mult)
+            nc.vector.scalar_tensor_tensor(excite[b][:, cols], y, 0.0, factor, ALU.max, ALU.mult)
 
         def masked_sum(b, cols, gg, accum):
             factor = decay[b][:, cols] if b < 2 else before23[:, b - 2, cols]
@@ -210,27 +211,26 @@ def tile_picked_yhawem_res_p_kernel(tc, x_words, x_scales, w1, e_words, e_scales
         quantise_h(0)
         for u in range(2):
             gather(ew_picked, ew, past_sb, u * HALF, (u + 1) * HALF)
-            second_product(0, half(u), y_half[0][u])
-        quantise_h(1)
-        for u in range(2):
-            second_product(1, half(u), y_half[1][u])
-        for b in range(2, BLOCKS):
+            second_product(0, half(u), y_half[u])
+        for b in range(1, BLOCKS):
             quantise_h(b)
             second_product(b, slice(0, V), y_ps[b])
         for b in range(3):
-            exp(b)
-        for b in range(2):
-            for u in range(2):
-                excitation(b, half(u), y_half[b][u])
+            exp(b, slice(0, V))
+        for u in range(2):
+            excitation(0, half(u), y_half[u][:])
+        excitation(1, slice(0, V), y_ps[1][:])
         masked_sum(0, slice(0, V + 1), gg_rows[:, 0, 0 : V + 1], total0[:])
         masked_sum(1, slice(0, V + 1), gg_rows[:, 1, 0 : V + 1], total1[:])
         nc.vector.reciprocal(plain_inverse0[:], total0[:])
-        excitation(2, slice(0, V), y_ps[2])
-        exp(3)
+        excitation(2, slice(0, V), y_ps[2][:])
+        nc.vector.reciprocal(plain_inverse1[:], total1[:])
+        for u in range(2):
+            exp(3, half(u))
         nc.scalar.activation(inverse[0], plain_inverse0[:], ACT.Copy, scale=OUT_FACTOR)
-        nc.scalar.activation(rate1[:], total1[:], ACT.Copy, scale=1.0 / OUT_FACTOR)
-        excitation(3, slice(0, V), y_ps[3])
-        nc.vector.reciprocal(inverse[1], rate1[:])
+        nc.scalar.activation(inverse[1], plain_inverse1[:], ACT.Copy, scale=OUT_FACTOR)
+        for u in range(2):
+            excitation(3, half(u), y_ps[3][:, half(u)])
         nc.scalar.copy(excite3[:, V : V + 1], mu_cols[:, 3 * MU_STEP : 3 * MU_STEP + 1])
         for b in range(2):
             scale_on_scalar(b, slice(0, V))

from contextlib import ExitStack

import concourse.mybir as mybir

F32 = mybir.dt.float32
BF16 = mybir.dt.bfloat16
I32 = mybir.dt.int32
U32 = mybir.dt.uint32
U16 = mybir.dt.uint16
U8 = mybir.dt.uint8
FP8X4 = mybir.dt.float8_e4m3fn_x4
ALU = mybir.AluOpType
ACT = mybir.ActivationFunctionType

P = 128
PACK = 4
QUADRANT = 32
QUADRANT_SCALES = 4
SCALE_ROWS = QUADRANT_SCALES * P // QUADRANT
WIDE_AT = P - SCALE_ROWS
LIST_ROWS = 16
K, H, S, V, T = 512, 512, 512, 512, 2048
BLOCKS = S // P
HALF = 256
PAD = 8
MU_STEP = 8
CAST_VECTOR = 88
DECAY_RATE, OUT_FACTOR = -0.7, 50.0
FLOPS = 2 * K * H * S + 2 * H * S * V

ROW = 4 * V
LAP = 64
BANK = 2048
W_CODES_AT = 0
ES_AT = W_CODES_AT + 4 * H
ES_PICKED_AT = ES_AT + T
AGO_AT = ES_PICKED_AT + 4 * HALF + 4 * P
LAST_EXCITE_AT = AGO_AT + BLOCKS * ROW + 2 * LAP
LAST_GG_AT = LAST_EXCITE_AT + ROW + LAP


def tile_picked_yhawem_res_p_kernel(tc, x_words, x_scales, w1, e_words, e_scales, ago, before, mu, offs, past, out):
    nc = tc.nc
    with ExitStack() as ctx:
        keep = ctx.enter_context(tc.tile_pool(name="keep", bufs=1))
        share = ctx.enter_context(tc.tile_pool(name="share", bufs=1))
        psum = ctx.enter_context(tc.psum_pool(name="psum", bufs=1))

        def events(b):
            return slice(b * P, (b + 1) * P)

        def half(u):
            return slice(u * HALF, (u + 1) * HALF)

        offs_sb = keep.tile([P, S // LIST_ROWS], U16, name="offs_sb")
        past_sb = keep.tile([P, V // LIST_ROWS], U16, name="past_sb")
        xw = keep.tile([P, T], U32, name="xw", align_bytes=64)
        ew = keep.tile([P, T], U32, name="ew", align_bytes=64)
        xs = keep.tile([P, T], U8, name="xs", align_bytes=64)
        es = share.tile([P, T], U8, name="es", align_bytes=64, offset=ES_AT)
        w_raw = keep.tile([P, PACK, H], F32, name="w_raw", align_bytes=64)
        ago_sb = [share.tile([P, V + (LAP // 2 if b == 3 else 0)], F32, name=f"ago{b}", align_bytes=64, offset=AGO_AT + ROW * b) for b in range(BLOCKS)]
        before01 = keep.tile([P, 2, V], F32, name="before01", align_bytes=64)
        before23 = keep.tile([P, 2, V + PAD], F32, name="before23", align_bytes=64)
        mu_rows = keep.tile([P, QUADRANT], F32, name="mu_rows", align_bytes=64)
        mu_cols = share.tile([P, QUADRANT], F32, name="mu_cols", align_bytes=64, offset=ES_AT)
        xs_picked = keep.tile([P, S], U8, name="xs_picked", align_bytes=64)
        es_picked = share.tile([P, V], U8, name="es_picked", align_bytes=64, offset=ES_PICKED_AT + 4 * HALF - LAP)
        xs_plane = keep.tile([P, S], U8, name="xs_plane", align_bytes=64)
        es_plane = keep.tile([P, V], U8, name="es_plane", align_bytes=64)
        ew_picked = keep.tile([P, V], U32, name="ew_picked", align_bytes=64)
        xw_picked = keep.tile([P, S], U32, name="xw_picked", align_bytes=64)
        w_bf = keep.tile([P, PACK, P, PACK], BF16, name="w_bf", align_bytes=64)
        w_codes = share.tile([P, H], U32, name="w_codes", align_bytes=64, offset=W_CODES_AT)
        w_scale = keep.tile([P, H], U8, name="w_scale", align_bytes=64)
        h_ps = [psum.tile([P, PACK, P], F32, name=f"h_ps{b}", offset=BANK * b) for b in range(BLOCKS)]
        y_half = [psum.tile([P, HALF], F32, name=f"y_half{u}", offset=BANK * BLOCKS * (1 - u)) for u in range(2)]
        y_ps = {b: psum.tile([P, V], F32, name=f"y_ps{b}", offset=BANK * (BLOCKS + b)) for b in range(1, BLOCKS)}
        h_bf = [keep.tile([P, P, PACK], BF16, name=f"h_bf{b}", align_bytes=64) for b in range(BLOCKS)]
        h_scale = keep.tile([P, S], U8, name="h_scale", align_bytes=64)
        h_codes_late = share.tile([P, BLOCKS - 1, P], U32, name="h_codes_late", align_bytes=64, offset=ES_PICKED_AT)
        h_codes = [keep.tile([P, P], U32, name="h_codes0", align_bytes=64)[:]]
        h_codes.extend(h_codes_late[:, b, :] for b in range(BLOCKS - 1))
        decay = [keep.tile([P, V + PAD], F32, name=f"decay{b}", align_bytes=64) for b in range(BLOCKS)]
        excite012 = keep.tile([P, BLOCKS - 1, V + PAD], F32, name="excite012", align_bytes=64)
        excite3 = share.tile([P, V + PAD], F32, name="excite3", align_bytes=64, offset=LAST_EXCITE_AT)
        excite = [excite012[:, 0, :], excite012[:, 1, :], excite012[:, 2, :], excite3[:]]
        gg_rows = keep.tile([P, BLOCKS, V + PAD], F32, name="gg_rows", align_bytes=64)
        gg_last = share.tile([P, HALF + PAD], F32, name="gg_last", align_bytes=64, offset=LAST_GG_AT)
        total0 = keep.tile([P, 1], F32, name="total0")
        total1 = keep.tile([P, 1], F32, name="total1")
        plain_inverse0 = share.tile([P, 1], F32, name="plain_inverse0", align_bytes=64, offset=AGO_AT + ROW)
        total2 = share.tile([P, 1], F32, name="total2", align_bytes=64, offset=LAST_GG_AT)
        total3 = keep.tile([P, 1], F32, name="total3")
        plain_inverse1 = share.tile([P, 1], F32, name="plain_inverse1", align_bytes=64, offset=AGO_AT + 2 * ROW)
        rate2 = keep.tile([P, 1], F32, name="rate2")
        inverse = [share.tile([P, 1], F32, name="inverse0", align_bytes=64, offset=AGO_AT + BLOCKS * ROW)[:]]
        inverse.append(share.tile([P, 1], F32, name="inverse1", align_bytes=64, offset=AGO_AT + BLOCKS * ROW + LAP)[:])
        inverse.extend(keep.tile([P, 1], F32, name=f"inverse{b}")[:] for b in (2, 3))
        result = [share.tile([P, V], F32, name="result0", align_bytes=64, offset=AGO_AT + 3 * ROW)]
        result.extend(keep.tile([P, V], F32, name=f"result{b}", align_bytes=64) for b in range(1, BLOCKS))

        nc.vector.memset(xs[0:WIDE_AT, :].bitcast(I32), 0)
        nc.vector.memset(es[0:WIDE_AT, :].bitcast(I32), 0)
        nc.vector.memset(xs_plane[:].bitcast(I32), 0)
        nc.vector.memset(es_plane[:].bitcast(I32), 0)
        nc.vector.memset(mu_rows[:], 0.0)
        nc.vector.memset(before23[:, :, V : V + 2], 1.0)
        for b in range(2):
            nc.vector.memset(decay[b][:, V : V + 1], 1.0)

        def load_words(tile, words, first, last):
            nc.sync.dma_start(tile[:, first:last].bitcast(I32), words[0].rearrange("p n j -> p (n j)").bitcast(I32)[:, first:last])

        def load_scales(tile, scales):
            nc.scalar.dma_start(tile[WIDE_AT:P, :].bitcast(I32), scales[0].bitcast(I32))

        def move_scales(plane, picked):
            for r in range(QUADRANT_SCALES):
                nc.sync.dma_start(plane[r:P:QUADRANT, :].bitcast(I32), picked[WIDE_AT + r : P : QUADRANT_SCALES, :].bitcast(I32))

        def load_ago(b):
            nc.sync.dma_start(ago_sb[b][:, 0:V], ago[events(b), :])

        def gather(picked, table, offsets, first, last):
            nc.vector.tensor_copy(picked[:, first:last], table[:].indirect(offsets[:, first // LIST_ROWS : last // LIST_ROWS]))

        def first_product(b):
            for t in range(PACK):
                nc.tensor.matmul_mx(
                    h_ps[b][:, t, :],
                    lhsT=w_codes[:, t * P : (t + 1) * P].bitcast(FP8X4),
                    lhsT_scale=w_scale[:, t * P : (t + 1) * P],
                    rhs=xw_picked[:, events(b)].bitcast(FP8X4),
                    rhs_scale=xs_plane[:, events(b)],
                    start=True,
                    stop=True,
                )

        def relu(b):
            nc.scalar.activation(
                h_bf[b][:].rearrange("p (c i) t -> p c t i", i=4),
                h_ps[b][:].rearrange("p t (c i) -> p c t i", i=4),
                ACT.Relu,
            )

        def quantise_h(b):
            nc.vector.quantize_mx(out=h_codes[b].bitcast(FP8X4), scales=h_scale[:, events(b)], in_=h_bf[b][:].rearrange("p n t -> p (n t)"))

        def second_product(b, cols, y):
            nc.tensor.matmul_mx(
                y[:],
                lhsT=h_codes[b].bitcast(FP8X4),
                lhsT_scale=h_scale[:, events(b)],
                rhs=ew_picked[:, cols].bitcast(FP8X4),
                rhs_scale=es_plane[:, cols],
                start=True,
                stop=True,
            )

        def exp(b, cols):
            nc.scalar.activation(decay[b][:, cols], ago_sb[b][:, cols], ACT.Exp, scale=DECAY_RATE)

        def excitation(b, cols, y):
            factor = before01[:, b, cols] if b < 2 else decay[b][:, cols]
            nc.vector.scalar_tensor_tensor(excite[b][:, cols], y, 0.0, factor, ALU.max, ALU.mult)

        def masked_sum(b, cols, gg, accum):
            factor = decay[b][:, cols] if b < 2 else before23[:, b - 2, cols]
            nc.vector.scalar_tensor_tensor(gg, excite[b][:, cols], 1.0, factor, ALU.mult, ALU.mult, accum_out=accum)

        def scale_on_scalar(b, cols):
            nc.scalar.activation(result[b][:, cols], gg_rows[:, b, cols], ACT.Copy, scale=inverse[b])
            nc.sync.dma_start(out[events(b), cols], result[b][:, cols])

        def scale_on_vector(b, cols, gg):
            nc.vector.tensor_scalar(result[b][:, cols], gg, inverse[b], OUT_FACTOR, ALU.mult, ALU.mult)
            nc.sync.dma_start(out[events(b), cols], result[b][:, cols])

        nc.sync.dma_start(offs_sb[:], offs)
        load_scales(xs, x_scales)
        nc.sync.dma_start(past_sb[:], past)
        load_scales(es, e_scales)
        nc.sync.dma_start(w_raw[:], w1.rearrange("(p j) c -> p j c", j=PACK))
        nc.sync.dma_start(mu_rows[0:P:MU_STEP, :], mu.rearrange("(b q j) o -> q b (j o)", b=BLOCKS, q=P // QUADRANT))
        load_words(xw, x_words, 0, T)
        gather(xs_picked, xs, offs_sb, 0, S)
        gather(es_picked, es, past_sb, 0, V)
        move_scales(xs_plane, xs_picked)
        load_words(ew, e_words, 0, T)

        w_src = w_raw[:].rearrange("p j (m t) -> p m j t", t=PACK)
        w_dst = w_bf[:].rearrange("p t m j -> p m j t")
        nc.vector.tensor_copy(w_dst[:, 0:CAST_VECTOR], w_src[:, 0:CAST_VECTOR])
        nc.scalar.copy(w_dst[:, CAST_VECTOR:P], w_src[:, CAST_VECTOR:P])
        move_scales(es_plane, es_picked)
        nc.sync.dma_start(before01[:], before[half(0), :].rearrange("(b p) v -> p b v", b=2))
        for b in range(BLOCKS):
            load_ago(b)
        nc.sync.dma_start(before23[:, :, 0:V], before[half(1), :].rearrange("(b p) v -> p b v", b=2))
        nc.vector.transpose(mu_cols[:], mu_rows[:])
        nc.vector.quantize_mx(out=w_codes[:].bitcast(FP8X4), scales=w_scale[:], in_=w_bf[:].rearrange("p t m j -> p (t m j)"))
        nc.scalar.copy(excite012[:, :, V], mu_cols[:, 0 : 3 * MU_STEP : MU_STEP])

        for first, last in ((0, P), (P, HALF), (HALF, S)):
            gather(xw_picked, xw, offs_sb, first, last)
        for b in range(BLOCKS):
            first_product(b)
        for b in range(BLOCKS):
            relu(b)
        quantise_h(0)
        for u in range(2):
            gather(ew_picked, ew, past_sb, u * HALF, (u + 1) * HALF)
            second_product(0, half(u), y_half[u])
        for b in range(1, BLOCKS):
            quantise_h(b)
            second_product(b, slice(0, V), y_ps[b])
        for b in range(3):
            exp(b, slice(0, V))
        for u in range(2):
            excitation(0, half(u), y_half[u][:])
        excitation(1, slice(0, V), y_ps[1][:])
        masked_sum(0, slice(0, V + 1), gg_rows[:, 0, 0 : V + 1], total0[:])
        masked_sum(1, slice(0, V + 1), gg_rows[:, 1, 0 : V + 1], total1[:])
        nc.vector.reciprocal(plain_inverse0[:], total0[:])
        excitation(2, slice(0, V), y_ps[2][:])
        nc.vector.reciprocal(plain_inverse1[:], total1[:])
        for u in range(2):
            exp(3, half(u))
        nc.scalar.activation(inverse[0], plain_inverse0[:], ACT.Copy, scale=OUT_FACTOR)
        nc.scalar.activation(inverse[1], plain_inverse1[:], ACT.Copy, scale=OUT_FACTOR)
        for u in range(2):
            excitation(3, half(u), y_ps[3][:, half(u)])
        nc.scalar.copy(excite3[:, V : V + 1], mu_cols[:, 3 * MU_STEP : 3 * MU_STEP + 1])
        for b in range(2):
            scale_on_scalar(b, slice(0, V))
        masked_sum(2, slice(0, V + 1), gg_rows[:, 2, 0 : V + 1], total2[:])
        masked_sum(3, half(0), gg_rows[:, 3, half(0)], excite3[:, V + 1 : V + 2])
        nc.scalar.activation(rate2[:], total2[:], ACT.Copy, scale=1.0 / OUT_FACTOR)
        nc.vector.reciprocal(inverse[2], rate2[:])
        masked_sum(3, slice(HALF, V + 2), gg_last[:, 0 : HALF + 2], total3[:])
        scale_on_scalar(2, half(0))
        nc.vector.tensor_scalar(result[2][:, half(1)], gg_rows[:, 2, half(1)], inverse[2], None, ALU.mult)
        nc.sync.dma_start(out[events(2), half(1)], result[2][:, half(1)])
        nc.vector.reciprocal(inverse[3], total3[:])
        scale_on_vector(3, half(0), gg_rows[:, 3, half(0)])
        scale_on_vector(3, half(1), gg_last[:, 0:HALF])
